import numpy as np
import ml_dtypes


def mxq(x, axis, fmt="e4m3"):
    dtype, down = {"e4m3": (ml_dtypes.float8_e4m3fn, 7), "e5m2": (ml_dtypes.float8_e5m2, 14)}[fmt]
    v = np.moveaxis(np.asarray(x, np.float32).astype(ml_dtypes.bfloat16).astype(np.float64), axis, -1)
    blocks = v.reshape(v.shape[:-1] + (-1, 32))
    amax = np.abs(blocks).max(-1, keepdims=True)
    byte = np.maximum(np.where(amax > 0, np.frexp(amax)[1] - 1 + 127, 0) - down, 1)
    scale = np.exp2(byte - 127.0)
    codes = (blocks / scale).astype(np.float32).astype(dtype).astype(np.float64)
    return np.moveaxis((codes * scale).reshape(v.shape), -1, axis)


WIDE = False


def mx_kscale(k):
    if not WIDE:
        return np.ones(k)
    levels = np.array([10, -10, 5, -5, 0])
    if k % 512:
        return np.exp2(np.random.permutation(np.resize(levels, k // 32))).repeat(32)
    a = np.empty((k // 512, 16))
    for p in range(k // 512):
        a[p, :8] = np.random.permutation(np.resize(levels, 8))
        for g in range(8):
            far = levels[np.abs(levels - a[p, g]) >= 10]
            a[p, g + 8] = far[np.random.randint(len(far))]
    return np.exp2(a.ravel()).repeat(32)


def f64(x):
    return np.asarray(x).astype(np.float64)


def striped(idx):
    return np.tile(idx.reshape(-1, 16).T, (8, 1)).astype(np.uint16)


def unstriped(offs):
    return offs[:16].T.reshape(-1).astype(np.int64)


E2M1 = np.array([0.0, 0.5, 1.0, 1.5, 2.0, 3.0, 4.0, 6.0, -0.0, -0.5, -1.0, -1.5, -2.0, -3.0, -4.0, -6.0])


def pack_weight(w, fmt):
    k, n = w.shape
    w = f64(np.asarray(w, np.float32).astype(ml_dtypes.bfloat16)).reshape(k // 32, 32, n)
    amax = np.abs(w).max(1)
    if fmt == "e4m3":
        byte = np.frexp(amax)[1] - 1 + 127 - 7
    else:
        mant, ex = np.frexp(amax / 6.0)
        byte = np.where(mant > 0.5, ex, ex - 1) + 127
    byte = np.clip(np.where(amax > 0, byte, 1), 1, 254)
    scaled = (w * np.exp2(127.0 - byte)[:, None, :]).reshape(k, n).astype(np.float32)
    by_word = np.ascontiguousarray(scaled.reshape(k // 512, 128, 4, n).transpose(0, 1, 3, 2))
    if fmt == "e4m3":
        words = by_word.astype(ml_dtypes.float8_e4m3fn).view(np.uint8)
    else:
        c = by_word.astype(ml_dtypes.float4_e2m1fn).view(np.uint8) & 0xF
        words = (c[..., 0::2] | (c[..., 1::2] << 4)).reshape(k // 512, 128, 2 * n)
    return np.ascontiguousarray(words), np.ascontiguousarray(byte.astype(np.uint8).reshape(k // 512, 16, n))


def unpack_weight(words, scales, fmt):
    g, _, n = scales.shape
    words = np.ascontiguousarray(words).reshape(g, 128, n, -1)
    if fmt == "e4m3":
        vals = words.view(ml_dtypes.float8_e4m3fn).astype(np.float64)
    else:
        nib = np.empty((g, 128, n, 4), np.uint8)
        nib[..., 0::2] = words & 0xF
        nib[..., 1::2] = words >> 4
        vals = E2M1[nib]
    vals = vals * np.repeat(np.exp2(scales.astype(np.float64) - 127.0), 8, axis=1)[..., None]
    return vals.transpose(0, 1, 3, 2).reshape(g * 512, n)


def gelu(v):
    return 0.5 * v * (1.0 + np.tanh(np.sqrt(2.0 / np.pi) * (v + 0.044715 * v**3)))


def striped8(idx):
    return np.concatenate([v.reshape(-1, 16).T for v in idx]).astype(np.uint16)


def unstriped8(offs):
    return np.stack([offs[16 * g:16 * g + 16].T.reshape(-1) for g in range(8)]).astype(np.int64)


def runs(v, idx8):
    k = np.arange(v.shape[0])
    return v[k[:, None], idx8[k % 512 // 64]]


K, K2, T, S, H, N = 1024, 512, 2048, 1024, 1024, 512

def setup_inputs():
    n = np.random.standard_normal
    s = mx_kscale(K)[:, None]
    s2 = mx_kscale(K2)[:, None]
    u = mx_kscale(H)[:, None]
    tab_words, tab_scales = pack_weight(n((K, T)) * s, "e4m3")
    tab2_words, tab2_scales = pack_weight(n((K2, T)) * s2, "e4m3")
    w4_words, w4_scales = pack_weight(n((K2, H)) / np.sqrt(K2) / s2, "e2m1")
    return {
        "tab_words": tab_words, "tab_scales": tab_scales,
        "tab2_words": tab2_words, "tab2_scales": tab2_scales,
        "offs": striped8(np.stack([np.random.permutation(T)[:S] for _ in range(8)])),
        "offs2": striped(np.random.permutation(T)[:S]),
        "w1": (n((K, H)) / np.sqrt(K) / s).astype(np.float32),
        "w4_words": w4_words, "w4_scales": w4_scales,
        "gain": (np.exp(0.3 * n(H)) * u[:, 0]).astype(np.float32),
        "w3": (n((H, N)) / np.sqrt(H) / u).astype(np.float32),
    }

def reference(tab_words, tab_scales, tab2_words, tab2_scales, offs, offs2, w1, w4_words, w4_scales, gain, w3):
    v = runs(unpack_weight(tab_words, tab_scales, "e4m3"), unstriped8(offs))
    v2 = unpack_weight(tab2_words, tab2_scales, "e4m3")[:, unstriped(offs2)]
    a = mxq(f64(w1), 0, "e4m3").T @ v
    b = unpack_weight(w4_words, w4_scales, "e2m1").T @ v2
    d = np.maximum(a, b) - np.minimum(a, b)
    act = 0.5 * d * (1.0 + np.tanh(np.sqrt(2.0 / np.pi) * (d + 0.044715 * d * d * d)))
    h = f64(gain)[:, None] * act
    y = mxq(f64(w3), 0, "e4m3").T @ mxq(h, 0, "e4m3")
    return y / (1.0 + np.exp(-y))

@@ -1,0 +1,293 @@
+from contextlib import ExitStack
+
+import concourse.mybir as mybir
+from concourse.masks import make_identity
+
+K, K2, T, S, H, N = 1024, 512, 2048, 1024, 1024, 512
+FLOPS = 2 * S * (K * H + K2 * H + H * N)
+
+F32 = mybir.dt.float32
+BF16 = mybir.dt.bfloat16
+I32 = mybir.dt.int32
+U32 = mybir.dt.uint32
+U16 = mybir.dt.uint16
+U8 = mybir.dt.uint8
+FP8X4 = mybir.dt.float8_e4m3fn_x4
+FP4X4 = mybir.dt.float4_e2m1fn_x4
+ACT = mybir.ActivationFunctionType
+ALU = mybir.AluOpType
+
+P = 128
+W = 512
+
+
+def tile_list_mould_cycle_gap_kernel(
+    tc, tab_words, tab_scales, tab2_words, tab2_scales, offs, offs2, w1, w4_words, w4_scales, gain, w3, out
+):
+    nc = tc.nc
+    with ExitStack() as ctx:
+        keep = ctx.enter_context(tc.tile_pool(name="keep", bufs=1))
+        ring = ctx.enter_context(tc.tile_pool(name="ring", bufs=2))
+        wide = ctx.enter_context(tc.tile_pool(name="wide", bufs=1))
+        psum = ctx.enter_context(tc.psum_pool(name="psum", bufs=1))
+
+        def held(shape, dtype, name):
+            return keep.tile(shape, dtype, name=name, align_bytes=64)
+
+        list8 = keep.tile([P, S // 16], U16, name="list8")
+        list1 = keep.tile([P, S // 16], U16, name="list1")
+        def big(shape, dtype, name, slot, skip=0):
+            return wide.tile(shape, dtype, name=name, offset=int(9216 * slot) + skip, align_bytes=64)
+
+        def bank(shape, name, index):
+            return psum.tile(shape, F32, name=name, offset=2048 * index)
+
+        ts_win = held([P, T], U8, "ts_win")
+        t2s_win = held([P, T], U8, "t2s_win")
+        w4_raw = held([P, 2 * H], U8, "w4_raw")
+        w4s_raw = held([P, H], U8, "w4s_raw")
+        gain_rows = held([P, P], F32, "gain_rows")
+        ident = held([P, P], F32, "ident")
+        w1_raw = {}
+        w3_raw = {}
+
+        nc.vector.memset(ts_win[:].bitcast(I32), 0)
+        nc.vector.memset(t2s_win[:].bitcast(I32), 0)
+        nc.gpsimd.memset(w4s_raw[:].bitcast(I32), 0)
+        nc.vector.memset(gain_rows[:], 0.0)
+        make_identity(nc, ident[:])
+        warm = held([P, 1], F32, "warm")
+        nc.scalar.activation(out=warm[:], in_=ident[:, 0:1], func=ACT.Gelu_apprx_tanh)
+
+        def words(ap):
+            return ap.rearrange("p t i -> p (t i)").bitcast(I32)
+
+        def load_table(src, name, slot):
+            window = big([P, T], U32, name, slot)
+            nc.sync.dma_start(out=window[:].bitcast(I32), in_=words(src))
+            return window
+
+        def load_w1(a, b, slot, skip=0):
+            w1_raw[a, b] = big([P, 4, W], F32, "w1_raw%d%d" % (a, b), slot, skip)
+            rows = w1[W * a : W * (a + 1), W * b : W * (b + 1)]
+            nc.sync.dma_start(out=w1_raw[a, b][:], in_=rows.rearrange("(p j) c -> p j c", j=4))
+
+        def load_plane(queue, dst, rows):
+            for d in range(4):
+                queue.dma_start(out=dst[32 * d : 32 * d + 4, :].bitcast(I32), in_=rows[4 * d : 4 * d + 4, :].bitcast(I32))
+
+        nc.sync.dma_start(list8[:], offs)
+        nc.sync.dma_start(list1[:], offs2)
+        nc.sync.dma_start(out=w4_raw[:].bitcast(I32), in_=w4_words[0].bitcast(I32))
+        ts_rows = tab_scales.bitcast(I32).rearrange("a (g c) t -> c g a t", c=2)
+        for c in range(2):
+            nc.sync.dma_start(out=ts_win[c:P:8, :].bitcast(I32), in_=ts_rows[c])
+        tab_sb = [load_table(tab_words[0], "tab0", 0)]
+        load_plane(nc.sync, t2s_win, tab2_scales[0])
+        tab_sb.append(load_table(tab_words[1], "tab1", 1))
+        load_w1(0, 0, 2)
+        load_plane(nc.gpsimd, w4s_raw, w4_scales[0])
+        gain_view = gain.rearrange("(b m t i) -> b t m i", b=2, t=4, i=4)
+        for b in range(2):
+            nc.gpsimd.dma_start(out=gain_rows[4 * b : 4 * b + 4, :].rearrange("t (m i) -> t m i", i=4), in_=gain_view[b])
+
+        w4_codes = held([P, 2 * H], U8, "w4_codes")
+        nc.vector.tensor_copy(
+            w4_codes[:].bitcast(I32).rearrange("p (b t m x) -> p b t m x", b=2, t=4, x=2),
+            w4_raw[:].bitcast(I32).rearrange("p (b m t x) -> p b t m x", b=2, t=4, x=2),
+        )
+        ts_got = held([P, S], U8, "ts_got")
+        ts_plane = held([P, S], U8, "ts_plane")
+        nc.vector.tensor_copy(ts_got[:], ts_win[:].indirect(list8[:]))
+        nc.vector.tensor_copy(ts_plane[:].bitcast(I32), ts_got[:].bitcast(I32))
+        for a in range(2):
+            for c in range(2):
+                nc.scalar.dma_start(
+                    out=ts_plane[8 * a + 2 + c : P : 32, :].bitcast(I32),
+                    in_=ts_got[16 + 8 * a + c : P : 32, :].bitcast(I32),
+                )
+        load_w1(1, 0, 3)
+        tab2_sb = load_table(tab2_words[0], "tab2", 4)
+        v_got = [held([P, S], U32, "v_got%d" % a) for a in range(2)]
+        nc.vector.tensor_copy(v_got[0][:], tab_sb[0][:].indirect(list8[:]))
+        load_w1(0, 1, 0)
+        w3_view = w3.rearrange("(b m t i) n -> b t m i n", b=2, t=4, i=4)
+
+        def load_w3(b, slot, skip):
+            w3_raw[b] = big([P, 4, N], F32, "w3_raw%d" % b, slot, skip)
+            for t in range(4):
+                nc.sync.dma_start(out=w3_raw[b][:, t, :], in_=w3_view[b, t])
+
+        nc.vector.tensor_copy(v_got[1][:], tab_sb[1][:].indirect(list8[:]))
+        load_w1(1, 1, 1, 1024)
+        w4_plane = big([P, H], U8, "w4_plane", 1)
+        t2s_plane = held([P, S], U8, "t2s_plane")
+        nc.vector.tensor_copy(t2s_plane[:], t2s_win[:].indirect(list1[:]))
+        nc.vector.tensor_copy(
+            w4_plane[:].bitcast(I32).rearrange("p (b t m) -> p b t m", b=2, t=4),
+            w4s_raw[:].bitcast(I32).rearrange("p (b m t) -> p b t m", b=2, t=4),
+        )
+
+
+        def quantise(name, grouped):
+            codes = held([P, W], U32, name + "_codes")
+            plane = held([P, W], U8, name + "_plane")
+            nc.vector.quantize_mx(out=codes[:].bitcast(FP8X4), scales=plane[:], in_=grouped[:])
+            return codes, plane
+
+        def prepare_w1(a, b, on_scalar):
+            if b == 0:
+                grouped = held([P, 4 * W], BF16, "w1_bf%d%d" % (a, b))
+            else:
+                grouped = big([P, 4 * W], BF16, "chain", 4)
+            src = w1_raw[a, b][:].rearrange("p j (m t i) -> p t m j i", t=4, i=4)
+            dst = grouped[:].rearrange("p (t m i j) -> p t m j i", t=4, i=4, j=4)
+            for t in range(4):
+                if on_scalar:
+                    nc.scalar.activation(out=dst[:, t], in_=src[:, t], func=ACT.Copy, scale=-1.0)
+                else:
+                    nc.vector.tensor_scalar(dst[:, t], src[:, t], -1.0, None, ALU.mult)
+            return quantise("w1_%d%d" % (a, b), grouped)
+
+        def prepare_w3(b):
+            grouped = big([P, 4 * N], BF16, "chain", 4)
+            nc.vector.tensor_copy(
+                grouped[:].rearrange("p (c i t) -> p c t i", i=4, t=4),
+                w3_raw[b][:].rearrange("p t (c i) -> p c t i", i=4),
+            )
+            return quantise("w3_%d" % b, grouped)
+
+        w1_q = {}
+        w1_q[0, 0] = prepare_w1(0, 0, True)
+        load_w3(0, 2, 0)
+        w1_q[1, 0] = prepare_w1(1, 0, True)
+        load_w3(1, 3, 0)
+        gain_ps = bank([P, 4 * W], "gain_ps", 4)
+        nc.tensor.transpose(gain_ps[:, 0:P], gain_rows[:], ident[:])
+        gain_col = held([P, 8], F32, "w1_bf10")
+        nc.vector.tensor_copy(gain_col[:], gain_ps[:, 0:8])
+
+        v2_got = [held([P, W], U32, "v2_got%d" % jh) for jh in range(2)]
+        for jh in range(2):
+            nc.vector.tensor_copy(v2_got[jh][:], tab2_sb[:].indirect(list1[:, 32 * jh : 32 * (jh + 1)]))
+
+        h_q = {}
+        gaps = {}
+
+        def first_products(b, jh, t):
+            cols = slice(W * jh, W * (jh + 1))
+            acc = bank([P, W], "gap_ps%d%d%d" % (b, jh, t), 4 * jh + t)
+            rows = slice(P * t, P * (t + 1))
+            for a in range(2):
+                codes, plane = w1_q[a, b]
+                nc.tensor.matmul_mx(
+                    out=acc[:],
+                    lhsT=codes[:, rows].bitcast(FP8X4),
+                    lhsT_scale=plane[:, rows],
+                    rhs=v_got[a][:, cols].bitcast(FP8X4),
+                    rhs_scale=ts_plane[8 * a : P, cols],
+                    start=(a == 0),
+                    stop=False,
+                )
+            r0 = W * b + P * t
+            nc.tensor.matmul_mx(
+                out=acc[:],
+                lhsT=w4_codes[:, 2 * r0 : 2 * (r0 + P)].bitcast(FP4X4),
+                lhsT_scale=w4_plane[:, r0 : r0 + P],
+                rhs=v2_got[jh][:].bitcast(FP8X4),
+                rhs_scale=t2s_plane[:, cols],
+                start=False,
+                stop=True,
+            )
+            return acc
+
+        def hidden_shared(b, jh, on_vector):
+            gap = held([P, 4, W], F32, "gap%d%d" % (b, jh))
+            gaps[b, jh] = gap
+            act = ring.tile([P, 4, W], F32, name="act", align_bytes=64)
+            for t in range(4):
+                acc = first_products(b, jh, t)
+                if t in on_vector:
+                    nc.scalar.activation(out=gap[:, t, :], in_=acc[:], func=ACT.Gelu_apprx_tanh, scale=-1.0)
+                    nc.vector.scalar_tensor_tensor(act[:, t, :], acc[:], 0.0, gap[:, t, :], ALU.max, ALU.add)
+                else:
+                    nc.scalar.activation(out=gap[:, t, :], in_=acc[:], func=ACT.Abs)
+                    nc.scalar.activation(out=act[:, t, :], in_=gap[:, t, :], func=ACT.Gelu_apprx_tanh)
+            grouped = big([P, 4 * W], BF16, "chain", 4)
+            nc.vector.tensor_tensor(
+                grouped[:].rearrange("p (c i t) -> p c t i", i=4, t=4),
+                act[:].rearrange("p t (c i) -> p c t i", i=4),
+                gain_col[:, 4 * b : 4 * b + 4].unsqueeze(1).unsqueeze(3).to_broadcast([P, W // 4, 4, 4]),
+                ALU.mult,
+            )
+            h_q[b, jh] = quantise("h_%d%d" % (b, jh), grouped)
+
+        def hidden(b, jh, pieces):
+            gap = held([P, 4, W], F32, "gap%d%d" % (b, jh))
+            gaps[b, jh] = gap
+            banks = [first_products(b, jh, t) for t in range(4)]
+            act = ring.tile([P, 2, W, 2], F32, name="act", align_bytes=64)
+            grouped = big([P, W, 4], BF16, "chain", 4)
+            codes = held([P, W], U32, "h_codes%d%d" % (b, jh))
+            plane = held([P, W], U8, "h_plane%d%d" % (b, jh))
+            width = W // pieces
+            for piece in range(pieces):
+                n = slice(width * piece, width * (piece + 1))
+                for u in range(2):
+                    for t in (2 * u, 2 * u + 1):
+                        nc.scalar.activation(out=gap[:, t, n], in_=banks[t][:, n], func=ACT.Abs)
+                    nc.scalar.activation(
+                        out=act[:, u, n, :],
+                        in_=gap[:, 2 * u : 2 * u + 2, n].rearrange("p e n -> p n e"),
+                        func=ACT.Gelu_apprx_tanh,
+                    )
+                nc.vector.tensor_tensor(
+                    grouped[:, n, :].rearrange("p n (u e) -> p n u e", e=2),
+                    act[:, :, n, :].rearrange("p u n e -> p n u e"),
+                    gain_col[:, 4 * b : 4 * b + 4].rearrange("p (u e) -> p u e", e=2).unsqueeze(1).to_broadcast([P, width, 2, 2]),
+                    ALU.mult,
+                )
+                nc.vector.quantize_mx(
+                    out=codes[:, n].bitcast(FP8X4), scales=plane[:, n], in_=grouped[:, n, :].rearrange("p n t -> p (n t)")
+                )
+            h_q[b, jh] = codes, plane
+
+        def codes_out(jh, c0, width, staged):
+            per_bank = W // width
+            cols = slice(c0, c0 + width)
+            for n0 in range(0, 4, per_bank):
+                acc = bank([P, per_bank, width], "y_ps%d%d%d" % (jh, c0, n0), 4 * jh + (c0 // width) * (4 // per_bank) + n0 // per_bank)
+                for x in range(per_bank):
+                    rows = slice(P * (n0 + x), P * (n0 + x + 1))
+                    for b in range(2):
+                        nc.tensor.matmul_mx(
+                            out=acc[:, x, :],
+                            lhsT=w3_q[b][0][:, rows].bitcast(FP8X4),
+                            lhsT_scale=w3_q[b][1][:, rows],
+                            rhs=h_q[b, jh][0][:, cols].bitcast(FP8X4),
+                            rhs_scale=h_q[b, jh][1][:, cols],
+                            start=(b == 0),
+                            stop=(b == 1),
+                        )
+                part = staged[:, width * n0 : width * n0 + W]
+                nc.scalar.activation(out=part, in_=acc[:].rearrange("p x n -> p (x n)"), func=ACT.Silu)
+                dst = out[P * n0 : P * (n0 + per_bank), W * jh + c0 : W * jh + c0 + width]
+                nc.sync.dma_start(out=dst.rearrange("(x p) n -> p x n", p=P), in_=part.rearrange("p (x n) -> p x n", n=width))
+
+        w1_q[0, 1] = prepare_w1(0, 1, False)
+        w1_q[1, 1] = prepare_w1(1, 1, False)
+        hidden_shared(0, 0, (2, 3))
+        w3_q = [prepare_w3(0)]
+        hidden(0, 1, 1)
+        w3_q.append(prepare_w3(1))
+        hidden(1, 0, 1)
+        hidden(1, 1, 2)
+        probe = held([P, 1], F32, "probe")
+        nc.gpsimd.tensor_copy(probe[:].bitcast(I32), v2_got[0][:].bitcast(I32)[:, 0:1])
+        probe2 = held([P, 1], I32, "probe2")
+        nc.gpsimd.tensor_copy(probe2[:], w1_q[1, 1][0][:].bitcast(I32)[:, 0:1])
+        staged = held([P, 4 * W], F32, "gap11")
+        codes_out(0, 0, W, staged[:])
+        last = gaps[1, 0][:].rearrange("p t n -> p (t n)")
+        for half in range(2):
+            codes_out(1, 256 * half, 256, last[:, 1024 * half : 1024 * (half + 1)])

@@ -120,14 +120,8 @@ def tile_list_mould_cycle_gap_kernel(
 
         nc.vector.tensor_copy(v_got[1][:], tab_sb[1][:].indirect(list8[:]))
         load_w1(1, 1, 1, 1024)
-        w4_plane = big([P, H], U8, "w4_plane", 1)
         t2s_plane = held([P, S], U8, "t2s_plane")
         nc.vector.tensor_copy(t2s_plane[:], t2s_win[:].indirect(list1[:]))
-        nc.vector.tensor_copy(
-            w4_plane[:].bitcast(I32).rearrange("p (b t m) -> p b t m", b=2, t=4),
-            w4s_raw[:].bitcast(I32).rearrange("p (b m t) -> p b t m", b=2, t=4),
-        )
-
 
         def quantise(name, grouped):
             codes = held([P, W], U32, name + "_codes")
@@ -162,21 +156,28 @@ def tile_list_mould_cycle_gap_kernel(
         load_w3(0, 2, 0)
         w1_q[1, 0] = prepare_w1(1, 0, True)
         load_w3(1, 3, 0)
-        gain_ps = bank([P, 4 * W], "gain_ps", 4)
-        nc.tensor.transpose(gain_ps[:, 0:P], gain_rows[:], ident[:])
-        gain_col = held([P, 8], F32, "w1_bf10")
-        nc.vector.tensor_copy(gain_col[:], gain_ps[:, 0:8])
+        w4_plane = held([P, H], U8, "w1_bf10")
+        nc.vector.tensor_copy(
+            w4_plane[:].bitcast(I32).rearrange("p (b t m) -> p b t m", b=2, t=4),
+            w4s_raw[:].bitcast(I32).rearrange("p (b m t) -> p b t m", b=2, t=4),
+        )
 
         v2_got = [held([P, W], U32, "v2_got%d" % jh) for jh in range(2)]
         for jh in range(2):
             nc.vector.tensor_copy(v2_got[jh][:], tab2_sb[:].indirect(list1[:, 32 * jh : 32 * (jh + 1)]))
+        gain_col = big([P, 8], F32, "gain_col", 4, 4096)
+
+        def spread_gain():
+            gain_ps = bank([P, 5 * W], "gain_ps", 3)
+            nc.tensor.transpose(gain_ps[:, 0:P], gain_rows[:], ident[:])
+            nc.vector.tensor_copy(gain_col[:], gain_ps[:, 0:8])
 
         h_q = {}
         gaps = {}
 
         def first_products(b, jh, t):
             cols = slice(W * jh, W * (jh + 1))
-            acc = bank([P, W], "gap_ps%d%d%d" % (b, jh, t), 4 * jh + t)
+            acc = bank([P, W], "gap_ps%d%d%d" % (b, jh, t), 4 * jh + 3 - t)
             rows = slice(P * t, P * (t + 1))
             for a in range(2):
                 codes, plane = w1_q[a, b]
@@ -213,6 +214,8 @@ def tile_list_mould_cycle_gap_kernel(
                 else:
                     nc.scalar.activation(out=gap[:, t, :], in_=acc[:], func=ACT.Abs)
                     nc.scalar.activation(out=act[:, t, :], in_=gap[:, t, :], func=ACT.Gelu_apprx_tanh)
+                if t == 0:
+                    spread_gain()
             grouped = big([P, 4 * W], BF16, "chain", 4)
             nc.vector.tensor_tensor(
                 grouped[:].rearrange("p (c i t) -> p c t i", i=4, t=4),
@@ -282,10 +285,6 @@ def tile_list_mould_cycle_gap_kernel(
         w3_q.append(prepare_w3(1))
         hidden(1, 0, 1)
         hidden(1, 1, 2)
-        probe = held([P, 1], F32, "probe")
-        nc.gpsimd.tensor_copy(probe[:].bitcast(I32), v2_got[0][:].bitcast(I32)[:, 0:1])
-        probe2 = held([P, 1], I32, "probe2")
-        nc.gpsimd.tensor_copy(probe2[:], w1_q[1, 1][0][:].bitcast(I32)[:, 0:1])
         staged = held([P, 4 * W], F32, "gap11")
         codes_out(0, 0, W, staged[:])
         last = gaps[1, 0][:].rearrange("p t n -> p (t n)")

@@ -27,7 +27,7 @@ def tile_list_mould_cycle_gap_kernel(
     nc = tc.nc
     with ExitStack() as ctx:
         keep = ctx.enter_context(tc.tile_pool(name="keep", bufs=1))
-        ring = ctx.enter_context(tc.tile_pool(name="ring", bufs=2))
+        ring = ctx.enter_context(tc.tile_pool(name="ring", bufs=4))
         wide = ctx.enter_context(tc.tile_pool(name="wide", bufs=1))
         psum = ctx.enter_context(tc.psum_pool(name="psum", bufs=1))
 
@@ -38,6 +38,9 @@ def tile_list_mould_cycle_gap_kernel(
         list1 = keep.tile([P, S // 16], U16, name="list1")
         def big(shape, dtype, name, slot, skip=0):
             return wide.tile(shape, dtype, name=name, offset=int(9216 * slot) + skip, align_bytes=64)
+
+        def chain(shape, side):
+            return big(shape, BF16, "chain%d" % side, 4, 4096 * side)
 
         def bank(shape, name, index):
             return psum.tile(shape, F32, name=name, offset=2048 * index)
@@ -102,7 +105,7 @@ def tile_list_mould_cycle_gap_kernel(
         nc.vector.tensor_copy(ts_plane[:].bitcast(I32), ts_got[:].bitcast(I32))
         for a in range(2):
             for c in range(2):
-                nc.scalar.dma_start(
+                nc.sync.dma_start(
                     out=ts_plane[8 * a + 2 + c : P : 32, :].bitcast(I32),
                     in_=ts_got[16 + 8 * a + c : P : 32, :].bitcast(I32),
                 )
@@ -110,7 +113,6 @@ def tile_list_mould_cycle_gap_kernel(
         tab2_sb = load_table(tab2_words[0], "tab2", 4)
         v_got = [held([P, S], U32, "v_got%d" % a) for a in range(2)]
         nc.vector.tensor_copy(v_got[0][:], tab_sb[0][:].indirect(list8[:]))
-        load_w1(0, 1, 0)
         w3_view = w3.rearrange("(b m t i) n -> b t m i n", b=2, t=4, i=4)
 
         def load_w3(b, slot, skip):
@@ -119,9 +121,9 @@ def tile_list_mould_cycle_gap_kernel(
                 nc.sync.dma_start(out=w3_raw[b][:, t, :], in_=w3_view[b, t])
 
         nc.vector.tensor_copy(v_got[1][:], tab_sb[1][:].indirect(list8[:]))
-        load_w1(1, 1, 1, 1024)
-        t2s_plane = held([P, S], U8, "t2s_plane")
-        nc.vector.tensor_copy(t2s_plane[:], t2s_win[:].indirect(list1[:]))
+        load_w1(0, 1, 1)
+        t2s_plane = [held([P, W], U8, "t2s_plane0")]
+        nc.vector.tensor_copy(t2s_plane[0][:], t2s_win[:].indirect(list1[:, 0:32]))
 
         def quantise(name, grouped):
             codes = held([P, W], U32, name + "_codes")
@@ -131,9 +133,9 @@ def tile_list_mould_cycle_gap_kernel(
 
         def prepare_w1(a, b, on_scalar):
             if b == 0:
-                grouped = held([P, 4 * W], BF16, "w1_bf%d%d" % (a, b))
+                grouped = big([P, 4 * W], BF16, "w1_bf%d%d" % (a, b), 5, 4096 * a)
             else:
-                grouped = big([P, 4 * W], BF16, "chain", 4)
+                grouped = chain([P, 4 * W], a)
             src = w1_raw[a, b][:].rearrange("p j (m t i) -> p t m j i", t=4, i=4)
             dst = grouped[:].rearrange("p (t m i j) -> p t m j i", t=4, i=4, j=4)
             for t in range(4):
@@ -144,7 +146,7 @@ def tile_list_mould_cycle_gap_kernel(
             return quantise("w1_%d%d" % (a, b), grouped)
 
         def prepare_w3(b):
-            grouped = big([P, 4 * N], BF16, "chain", 4)
+            grouped = chain([P, 4 * N], 1)
             nc.vector.tensor_copy(
                 grouped[:].rearrange("p (c i t) -> p c t i", i=4, t=4),
                 w3_raw[b][:].rearrange("p t (c i) -> p c t i", i=4),
@@ -153,19 +155,21 @@ def tile_list_mould_cycle_gap_kernel(
 
         w1_q = {}
         w1_q[0, 0] = prepare_w1(0, 0, True)
-        load_w3(0, 2, 0)
+        load_w1(1, 1, 2)
         w1_q[1, 0] = prepare_w1(1, 0, True)
-        load_w3(1, 3, 0)
-        w4_plane = held([P, H], U8, "w1_bf10")
+        load_w3(0, 3, 0)
+        w4_plane = big([P, H], U8, "w4_plane", 5, 4096)
         nc.vector.tensor_copy(
             w4_plane[:].bitcast(I32).rearrange("p (b t m) -> p b t m", b=2, t=4),
             w4s_raw[:].bitcast(I32).rearrange("p (b m t) -> p b t m", b=2, t=4),
         )
 
         v2_got = [held([P, W], U32, "v2_got%d" % jh) for jh in range(2)]
-        for jh in range(2):
-            nc.vector.tensor_copy(v2_got[jh][:], tab2_sb[:].indirect(list1[:, 32 * jh : 32 * (jh + 1)]))
-        gain_col = big([P, 8], F32, "gain_col", 4, 4096)
+        nc.vector.tensor_copy(v2_got[0][:], tab2_sb[:].indirect(list1[:, 0:32]))
+        t2s_plane.append(big([P, W], U8, "t2s_plane1", 5, 4096 + H))
+        nc.vector.tensor_copy(t2s_plane[1][:], t2s_win[:].indirect(list1[:, 32:64]))
+        nc.vector.tensor_copy(v2_got[1][:], tab2_sb[:].indirect(list1[:, 32:64]))
+        gain_col = held([P, 8], F32, "gain_col")
 
         def spread_gain():
             gain_ps = bank([P, 5 * W], "gain_ps", 3)
@@ -196,41 +200,18 @@ def tile_list_mould_cycle_gap_kernel(
                 lhsT=w4_codes[:, 2 * r0 : 2 * (r0 + P)].bitcast(FP4X4),
                 lhsT_scale=w4_plane[:, r0 : r0 + P],
                 rhs=v2_got[jh][:].bitcast(FP8X4),
-                rhs_scale=t2s_plane[:, cols],
+                rhs_scale=t2s_plane[jh][:],
                 start=False,
                 stop=True,
             )
             return acc
-
-        def hidden_shared(b, jh, on_vector):
-            gap = held([P, 4, W], F32, "gap%d%d" % (b, jh))
-            gaps[b, jh] = gap
-            act = ring.tile([P, 4, W], F32, name="act", align_bytes=64)
-            for t in range(4):
-                acc = first_products(b, jh, t)
-                if t in on_vector:
-                    nc.scalar.activation(out=gap[:, t, :], in_=acc[:], func=ACT.Gelu_apprx_tanh, scale=-1.0)
-                    nc.vector.scalar_tensor_tensor(act[:, t, :], acc[:], 0.0, gap[:, t, :], ALU.max, ALU.add)
-                else:
-                    nc.scalar.activation(out=gap[:, t, :], in_=acc[:], func=ACT.Abs)
-                    nc.scalar.activation(out=act[:, t, :], in_=gap[:, t, :], func=ACT.Gelu_apprx_tanh)
-                if t == 0:
-                    spread_gain()
-            grouped = big([P, 4 * W], BF16, "chain", 4)
-            nc.vector.tensor_tensor(
-                grouped[:].rearrange("p (c i t) -> p c t i", i=4, t=4),
-                act[:].rearrange("p t (c i) -> p c t i", i=4),
-                gain_col[:, 4 * b : 4 * b + 4].unsqueeze(1).unsqueeze(3).to_broadcast([P, W // 4, 4, 4]),
-                ALU.mult,
-            )
-            h_q[b, jh] = quantise("h_%d%d" % (b, jh), grouped)
 
         def hidden(b, jh, pieces):
             gap = held([P, 4, W], F32, "gap%d%d" % (b, jh))
             gaps[b, jh] = gap
             banks = [first_products(b, jh, t) for t in range(4)]
             act = ring.tile([P, 2, W, 2], F32, name="act", align_bytes=64)
-            grouped = big([P, W, 4], BF16, "chain", 4)
+            grouped = chain([P, W, 4], b * jh)
             codes = held([P, W], U32, "h_codes%d%d" % (b, jh))
             plane = held([P, W], U8, "h_plane%d%d" % (b, jh))
             width = W // pieces
@@ -244,6 +225,8 @@ def tile_list_mould_cycle_gap_kernel(
                         in_=gap[:, 2 * u : 2 * u + 2, n].rearrange("p e n -> p n e"),
                         func=ACT.Gelu_apprx_tanh,
                     )
+                if (b, jh) == (0, 0):
+                    spread_gain()
                 nc.vector.tensor_tensor(
                     grouped[:, n, :].rearrange("p n (u e) -> p n u e", e=2),
                     act[:, :, n, :].rearrange("p u n e -> p n u e"),
@@ -278,8 +261,9 @@ def tile_list_mould_cycle_gap_kernel(
                 nc.sync.dma_start(out=dst.rearrange("(x p) n -> p x n", p=P), in_=part.rearrange("p (x n) -> p x n", n=width))
 
         w1_q[0, 1] = prepare_w1(0, 1, False)
+        load_w3(1, 1, 0)
         w1_q[1, 1] = prepare_w1(1, 1, False)
-        hidden_shared(0, 0, (2, 3))
+        hidden(0, 0, 1)
         w3_q = [prepare_w3(0)]
         hidden(0, 1, 1)
         w3_q.append(prepare_w3(1))

@@ -19,6 +19,10 @@ ALU = mybir.AluOpType
 
 P = 128
 W = 512
+HALF_COLUMNS = W // 16
+BANK_BYTES = 4 * W
+ROOM_BYTES = 9216
+GROUPED_BYTES = 2 * 4 * W
 
 
 def tile_list_mould_cycle_gap_kernel(
@@ -28,102 +32,106 @@ def tile_list_mould_cycle_gap_kernel(
     with ExitStack() as ctx:
         keep = ctx.enter_context(tc.tile_pool(name="keep", bufs=1))
         ring = ctx.enter_context(tc.tile_pool(name="ring", bufs=4))
-        wide = ctx.enter_context(tc.tile_pool(name="wide", bufs=1))
+        rooms = ctx.enter_context(tc.tile_pool(name="rooms", bufs=1))
         psum = ctx.enter_context(tc.psum_pool(name="psum", bufs=1))
 
         def held(shape, dtype, name):
             return keep.tile(shape, dtype, name=name, align_bytes=64)
 
-        list8 = keep.tile([P, S // 16], U16, name="list8")
-        list1 = keep.tile([P, S // 16], U16, name="list1")
-        def big(shape, dtype, name, slot, skip=0):
-            return wide.tile(shape, dtype, name=name, offset=int(9216 * slot) + skip, align_bytes=64)
+        def tenant(shape, dtype, name, room, skip=0):
+            return rooms.tile(shape, dtype, name=name, offset=ROOM_BYTES * room + skip, align_bytes=64)
 
-        def chain(shape, side):
-            return big(shape, BF16, "chain%d" % side, 4, 4096 * side)
+        def late_grouped(shape, side):
+            return tenant(shape, BF16, "late_grouped%d" % side, 4, GROUPED_BYTES * side)
 
         def bank(shape, name, index):
-            return psum.tile(shape, F32, name=name, offset=2048 * index)
+            return psum.tile(shape, F32, name=name, offset=BANK_BYTES * index)
 
-        ts_win = held([P, T], U8, "ts_win")
-        t2s_win = held([P, T], U8, "t2s_win")
+        list8 = keep.tile([P, S // 16], U16, name="list8")
+        list1 = keep.tile([P, S // 16], U16, name="list1")
+        tab_scale_window = held([P, T], U8, "tab_scale_window")
+        tab2_scale_window = held([P, T], U8, "tab2_scale_window")
         w4_raw = held([P, 2 * H], U8, "w4_raw")
-        w4s_raw = held([P, H], U8, "w4s_raw")
+        w4_scale_raw = held([P, H], U8, "w4_scale_raw")
         gain_rows = held([P, P], F32, "gain_rows")
         ident = held([P, P], F32, "ident")
         w1_raw = {}
         w3_raw = {}
 
-        nc.vector.memset(ts_win[:].bitcast(I32), 0)
-        nc.vector.memset(t2s_win[:].bitcast(I32), 0)
-        nc.gpsimd.memset(w4s_raw[:].bitcast(I32), 0)
+        nc.vector.memset(tab_scale_window[:].bitcast(I32), 0)
+        nc.vector.memset(tab2_scale_window[:].bitcast(I32), 0)
+        nc.gpsimd.memset(w4_scale_raw[:].bitcast(I32), 0)
         nc.vector.memset(gain_rows[:], 0.0)
         make_identity(nc, ident[:])
-        warm = held([P, 1], F32, "warm")
-        nc.scalar.activation(out=warm[:], in_=ident[:, 0:1], func=ACT.Gelu_apprx_tanh)
+        zero_bias = held([P, 1], F32, "zero_bias")
+        nc.gpsimd.memset(zero_bias[:], 0.0)
+        nc.scalar.activation(out=zero_bias[:], in_=zero_bias[:], func=ACT.Gelu_apprx_tanh)
 
-        def words(ap):
-            return ap.rearrange("p t i -> p (t i)").bitcast(I32)
-
-        def load_table(src, name, slot):
-            window = big([P, T], U32, name, slot)
-            nc.sync.dma_start(out=window[:].bitcast(I32), in_=words(src))
+        def load_table(packed, name, room):
+            window = tenant([P, T], U32, name, room)
+            nc.sync.dma_start(out=window[:].bitcast(I32), in_=packed.rearrange("p t i -> p (t i)").bitcast(I32))
             return window
 
-        def load_w1(a, b, slot, skip=0):
-            w1_raw[a, b] = big([P, 4, W], F32, "w1_raw%d%d" % (a, b), slot, skip)
+        def load_w1(a, b, room):
+            w1_raw[a, b] = tenant([P, 4, W], F32, "w1_raw%d%d" % (a, b), room)
             rows = w1[W * a : W * (a + 1), W * b : W * (b + 1)]
             nc.sync.dma_start(out=w1_raw[a, b][:], in_=rows.rearrange("(p j) c -> p j c", j=4))
 
-        def load_plane(queue, dst, rows):
+        def load_w3(b, room):
+            w3_raw[b] = tenant([P, 4, N], F32, "w3_raw%d" % b, room)
+            rows = w3.rearrange("(b m t i) n -> b t m i n", b=2, t=4, i=4)
+            for t in range(4):
+                nc.sync.dma_start(out=w3_raw[b][:, t, :], in_=rows[b, t])
+
+        def load_plane(queue, plane, rows):
             for d in range(4):
-                queue.dma_start(out=dst[32 * d : 32 * d + 4, :].bitcast(I32), in_=rows[4 * d : 4 * d + 4, :].bitcast(I32))
+                queue.dma_start(
+                    out=plane[32 * d : 32 * d + 4, :].bitcast(I32), in_=rows[4 * d : 4 * d + 4, :].bitcast(I32)
+                )
 
         nc.sync.dma_start(list8[:], offs)
         nc.sync.dma_start(list1[:], offs2)
         nc.sync.dma_start(out=w4_raw[:].bitcast(I32), in_=w4_words[0].bitcast(I32))
-        ts_rows = tab_scales.bitcast(I32).rearrange("a (g c) t -> c g a t", c=2)
+        tab_scale_rows = tab_scales.bitcast(I32).rearrange("a (g c) t -> c g a t", c=2)
         for c in range(2):
-            nc.sync.dma_start(out=ts_win[c:P:8, :].bitcast(I32), in_=ts_rows[c])
-        tab_sb = [load_table(tab_words[0], "tab0", 0)]
-        load_plane(nc.sync, t2s_win, tab2_scales[0])
-        tab_sb.append(load_table(tab_words[1], "tab1", 1))
+            nc.sync.dma_start(out=tab_scale_window[c:P:8, :].bitcast(I32), in_=tab_scale_rows[c])
+        tab_windows = [load_table(tab_words[0], "tab_pass0", 0)]
+        load_plane(nc.sync, tab2_scale_window, tab2_scales[0])
+        tab_windows.append(load_table(tab_words[1], "tab_pass1", 1))
         load_w1(0, 0, 2)
-        load_plane(nc.gpsimd, w4s_raw, w4_scales[0])
+        load_plane(nc.gpsimd, w4_scale_raw, w4_scales[0])
         gain_view = gain.rearrange("(b m t i) -> b t m i", b=2, t=4, i=4)
         for b in range(2):
-            nc.gpsimd.dma_start(out=gain_rows[4 * b : 4 * b + 4, :].rearrange("t (m i) -> t m i", i=4), in_=gain_view[b])
+            nc.gpsimd.dma_start(
+                out=gain_rows[4 * b : 4 * b + 4, :].rearrange("t (m i) -> t m i", i=4), in_=gain_view[b]
+            )
 
         w4_codes = held([P, 2 * H], U8, "w4_codes")
         nc.vector.tensor_copy(
             w4_codes[:].bitcast(I32).rearrange("p (b t m x) -> p b t m x", b=2, t=4, x=2),
             w4_raw[:].bitcast(I32).rearrange("p (b m t x) -> p b t m x", b=2, t=4, x=2),
         )
-        ts_got = held([P, S], U8, "ts_got")
-        ts_plane = held([P, S], U8, "ts_plane")
-        nc.vector.tensor_copy(ts_got[:], ts_win[:].indirect(list8[:]))
-        nc.vector.tensor_copy(ts_plane[:].bitcast(I32), ts_got[:].bitcast(I32))
+
+        tab_scale_picked = held([P, S], U8, "tab_scale_picked")
+        tab_planes = held([P, S], U8, "tab_planes")
+        nc.vector.tensor_copy(tab_scale_picked[:], tab_scale_window[:].indirect(list8[:]))
+        nc.vector.tensor_copy(tab_planes[:].bitcast(I32), tab_scale_picked[:].bitcast(I32))
         for a in range(2):
             for c in range(2):
                 nc.sync.dma_start(
-                    out=ts_plane[8 * a + 2 + c : P : 32, :].bitcast(I32),
-                    in_=ts_got[16 + 8 * a + c : P : 32, :].bitcast(I32),
+                    out=tab_planes[8 * a + 2 + c : P : 32, :].bitcast(I32),
+                    in_=tab_scale_picked[16 + 8 * a + c : P : 32, :].bitcast(I32),
                 )
         load_w1(1, 0, 3)
-        tab2_sb = load_table(tab2_words[0], "tab2", 4)
-        v_got = [held([P, S], U32, "v_got%d" % a) for a in range(2)]
-        nc.vector.tensor_copy(v_got[0][:], tab_sb[0][:].indirect(list8[:]))
-        w3_view = w3.rearrange("(b m t i) n -> b t m i n", b=2, t=4, i=4)
+        tab2_window = load_table(tab2_words[0], "tab2", 4)
 
-        def load_w3(b, slot, skip):
-            w3_raw[b] = big([P, 4, N], F32, "w3_raw%d" % b, slot, skip)
-            for t in range(4):
-                nc.sync.dma_start(out=w3_raw[b][:, t, :], in_=w3_view[b, t])
-
-        nc.vector.tensor_copy(v_got[1][:], tab_sb[1][:].indirect(list8[:]))
+        tab_picked = [held([P, S], U32, "tab_picked%d" % a) for a in range(2)]
+        for a in range(2):
+            nc.vector.tensor_copy(tab_picked[a][:], tab_windows[a][:].indirect(list8[:]))
         load_w1(0, 1, 1)
-        t2s_plane = [held([P, W], U8, "t2s_plane0")]
-        nc.vector.tensor_copy(t2s_plane[0][:], t2s_win[:].indirect(list1[:, 0:32]))
+        list1_halves = [list1[:, HALF_COLUMNS * half : HALF_COLUMNS * (half + 1)] for half in range(2)]
+        tab2_planes = [held([P, W], U8, "tab2_plane0")]
+        nc.vector.tensor_copy(tab2_planes[0][:], tab2_scale_window[:].indirect(list1_halves[0]))
 
         def quantise(name, grouped):
             codes = held([P, W], U32, name + "_codes")
@@ -131,146 +139,156 @@ def tile_list_mould_cycle_gap_kernel(
             nc.vector.quantize_mx(out=codes[:].bitcast(FP8X4), scales=plane[:], in_=grouped[:])
             return codes, plane
 
-        def prepare_w1(a, b, on_scalar):
-            if b == 0:
-                grouped = big([P, 4 * W], BF16, "w1_bf%d%d" % (a, b), 5, 4096 * a)
-            else:
-                grouped = chain([P, 4 * W], a)
+        def prepare_w1(a, b, grouped, tiles_on_scalar):
             src = w1_raw[a, b][:].rearrange("p j (m t i) -> p t m j i", t=4, i=4)
             dst = grouped[:].rearrange("p (t m i j) -> p t m j i", t=4, i=4, j=4)
             for t in range(4):
-                if on_scalar:
+                if t < tiles_on_scalar:
                     nc.scalar.activation(out=dst[:, t], in_=src[:, t], func=ACT.Copy, scale=-1.0)
                 else:
                     nc.vector.tensor_scalar(dst[:, t], src[:, t], -1.0, None, ALU.mult)
             return quantise("w1_%d%d" % (a, b), grouped)
 
         def prepare_w3(b):
-            grouped = chain([P, 4 * N], 1)
+            grouped = late_grouped([P, 4 * N], 1)
             nc.vector.tensor_copy(
                 grouped[:].rearrange("p (c i t) -> p c t i", i=4, t=4),
                 w3_raw[b][:].rearrange("p t (c i) -> p c t i", i=4),
             )
             return quantise("w3_%d" % b, grouped)
 
-        w1_q = {}
-        w1_q[0, 0] = prepare_w1(0, 0, True)
+        w1_mx = {}
+        w1_mx[0, 0] = prepare_w1(0, 0, tenant([P, 4 * W], BF16, "w1_grouped0", 5), 4)
         load_w1(1, 1, 2)
-        w1_q[1, 0] = prepare_w1(1, 0, True)
-        load_w3(0, 3, 0)
-        w4_plane = big([P, H], U8, "w4_plane", 5, 4096)
+        w1_mx[1, 0] = prepare_w1(1, 0, tenant([P, 4 * W], BF16, "w1_grouped1", 5, GROUPED_BYTES), 2)
+        load_w3(0, 3)
+        w4_plane = tenant([P, H], U8, "w4_plane", 5, GROUPED_BYTES)
         nc.vector.tensor_copy(
             w4_plane[:].bitcast(I32).rearrange("p (b t m) -> p b t m", b=2, t=4),
-            w4s_raw[:].bitcast(I32).rearrange("p (b m t) -> p b t m", b=2, t=4),
+            w4_scale_raw[:].bitcast(I32).rearrange("p (b m t) -> p b t m", b=2, t=4),
         )
 
-        v2_got = [held([P, W], U32, "v2_got%d" % jh) for jh in range(2)]
-        nc.vector.tensor_copy(v2_got[0][:], tab2_sb[:].indirect(list1[:, 0:32]))
-        t2s_plane.append(big([P, W], U8, "t2s_plane1", 5, 4096 + H))
-        nc.vector.tensor_copy(t2s_plane[1][:], t2s_win[:].indirect(list1[:, 32:64]))
-        nc.vector.tensor_copy(v2_got[1][:], tab2_sb[:].indirect(list1[:, 32:64]))
-        gain_col = held([P, 8], F32, "gain_col")
+        tab2_picked = [held([P, W], U32, "tab2_picked%d" % half) for half in range(2)]
+        nc.vector.tensor_copy(tab2_picked[0][:], tab2_window[:].indirect(list1_halves[0]))
+        tab2_planes.append(tenant([P, W], U8, "tab2_plane1", 5, GROUPED_BYTES + H))
+        nc.vector.tensor_copy(tab2_planes[1][:], tab2_scale_window[:].indirect(list1_halves[1]))
+        nc.vector.tensor_copy(tab2_picked[1][:], tab2_window[:].indirect(list1_halves[1]))
+
+        gain_columns = held([P, 8], F32, "gain_columns")
 
         def spread_gain():
-            gain_ps = bank([P, 5 * W], "gain_ps", 3)
-            nc.tensor.transpose(gain_ps[:, 0:P], gain_rows[:], ident[:])
-            nc.vector.tensor_copy(gain_col[:], gain_ps[:, 0:8])
+            turned = bank([P, 5 * W], "gain_turned", 3)
+            nc.tensor.transpose(turned[:, 0:P], gain_rows[:], ident[:])
+            nc.vector.tensor_copy(gain_columns[:], turned[:, 0:8])
 
-        h_q = {}
-        gaps = {}
-
-        def first_products(b, jh, t):
-            cols = slice(W * jh, W * (jh + 1))
-            acc = bank([P, W], "gap_ps%d%d%d" % (b, jh, t), 4 * jh + 3 - t)
-            rows = slice(P * t, P * (t + 1))
+        def difference(b, half, t):
+            acc = bank([P, W], "difference%d%d%d" % (b, half, t), 4 * half + 3 - t)
+            entries = slice(W * half, W * (half + 1))
+            features = slice(P * t, P * (t + 1))
             for a in range(2):
-                codes, plane = w1_q[a, b]
+                codes, plane = w1_mx[a, b]
                 nc.tensor.matmul_mx(
                     out=acc[:],
-                    lhsT=codes[:, rows].bitcast(FP8X4),
-                    lhsT_scale=plane[:, rows],
-                    rhs=v_got[a][:, cols].bitcast(FP8X4),
-                    rhs_scale=ts_plane[8 * a : P, cols],
+                    lhsT=codes[:, features].bitcast(FP8X4),
+                    lhsT_scale=plane[:, features],
+                    rhs=tab_picked[a][:, entries].bitcast(FP8X4),
+                    rhs_scale=tab_planes[8 * a : P, entries],
                     start=(a == 0),
                     stop=False,
                 )
-            r0 = W * b + P * t
+            first = W * b + P * t
             nc.tensor.matmul_mx(
                 out=acc[:],
-                lhsT=w4_codes[:, 2 * r0 : 2 * (r0 + P)].bitcast(FP4X4),
-                lhsT_scale=w4_plane[:, r0 : r0 + P],
-                rhs=v2_got[jh][:].bitcast(FP8X4),
-                rhs_scale=t2s_plane[jh][:],
+                lhsT=w4_codes[:, 2 * first : 2 * (first + P)].bitcast(FP4X4),
+                lhsT_scale=w4_plane[:, first : first + P],
+                rhs=tab2_picked[half][:].bitcast(FP8X4),
+                rhs_scale=tab2_planes[half][:],
                 start=False,
                 stop=True,
             )
             return acc
 
-        def hidden(b, jh, pieces):
-            gap = held([P, 4, W], F32, "gap%d%d" % (b, jh))
-            gaps[b, jh] = gap
-            banks = [first_products(b, jh, t) for t in range(4)]
+        gaps = {}
+        acts = {}
+        h_mx = {}
+
+        def activate(b, half):
+            gap = held([P, 4, W], F32, "gap%d%d" % (b, half))
+            for t in range(4):
+                nc.scalar.activation(out=gap[:, t, :], in_=difference(b, half, t)[:], func=ACT.Abs)
             act = ring.tile([P, 2, W, 2], F32, name="act", align_bytes=64)
-            grouped = chain([P, W, 4], b * jh)
-            codes = held([P, W], U32, "h_codes%d%d" % (b, jh))
-            plane = held([P, W], U8, "h_plane%d%d" % (b, jh))
+            nc.scalar.activation(
+                out=act[:],
+                in_=gap[:].rearrange("p (u e) n -> p u n e", e=2),
+                func=ACT.Gelu_apprx_tanh,
+                bias=zero_bias[:],
+            )
+            gaps[b, half] = gap
+            acts[b, half] = act
+
+        def quantise_h(b, half, side, pieces):
+            grouped = late_grouped([P, W, 4], side)
+            codes = held([P, W], U32, "h_codes%d%d" % (b, half))
+            plane = held([P, W], U8, "h_plane%d%d" % (b, half))
             width = W // pieces
+            gains = gain_columns[:, 4 * b : 4 * b + 4].rearrange("p (u e) -> p u e", e=2)
             for piece in range(pieces):
                 n = slice(width * piece, width * (piece + 1))
-                for u in range(2):
-                    for t in (2 * u, 2 * u + 1):
-                        nc.scalar.activation(out=gap[:, t, n], in_=banks[t][:, n], func=ACT.Abs)
-                    nc.scalar.activation(
-                        out=act[:, u, n, :],
-                        in_=gap[:, 2 * u : 2 * u + 2, n].rearrange("p e n -> p n e"),
-                        func=ACT.Gelu_apprx_tanh,
-                    )
-                if (b, jh) == (0, 0):
-                    spread_gain()
                 nc.vector.tensor_tensor(
                     grouped[:, n, :].rearrange("p n (u e) -> p n u e", e=2),
-                    act[:, :, n, :].rearrange("p u n e -> p n u e"),
-                    gain_col[:, 4 * b : 4 * b + 4].rearrange("p (u e) -> p u e", e=2).unsqueeze(1).to_broadcast([P, width, 2, 2]),
+                    acts[b, half][:, :, n, :].rearrange("p u n e -> p n u e"),
+                    gains.unsqueeze(1).to_broadcast([P, width, 2, 2]),
                     ALU.mult,
                 )
                 nc.vector.quantize_mx(
-                    out=codes[:, n].bitcast(FP8X4), scales=plane[:, n], in_=grouped[:, n, :].rearrange("p n t -> p (n t)")
+                    out=codes[:, n].bitcast(FP8X4),
+                    scales=plane[:, n],
+                    in_=grouped[:, n, :].rearrange("p n t -> p (n t)"),
                 )
-            h_q[b, jh] = codes, plane
+            h_mx[b, half] = codes, plane
 
-        def codes_out(jh, c0, width, staged):
+        def defect_codes(half, start, width, first_bank, staged):
             per_bank = W // width
-            cols = slice(c0, c0 + width)
+            entries = slice(start, start + width)
             for n0 in range(0, 4, per_bank):
-                acc = bank([P, per_bank, width], "y_ps%d%d%d" % (jh, c0, n0), 4 * jh + (c0 // width) * (4 // per_bank) + n0 // per_bank)
-                for x in range(per_bank):
-                    rows = slice(P * (n0 + x), P * (n0 + x + 1))
-                    for b in range(2):
+                acc = bank([P, per_bank, width], "y%d%d%d" % (half, start, n0), first_bank + n0 // per_bank)
+                for b in range(2):
+                    for x in range(per_bank):
+                        rows = slice(P * (n0 + x), P * (n0 + x + 1))
                         nc.tensor.matmul_mx(
                             out=acc[:, x, :],
-                            lhsT=w3_q[b][0][:, rows].bitcast(FP8X4),
-                            lhsT_scale=w3_q[b][1][:, rows],
-                            rhs=h_q[b, jh][0][:, cols].bitcast(FP8X4),
-                            rhs_scale=h_q[b, jh][1][:, cols],
-                            start=(b == 0),
-                            stop=(b == 1),
+                            lhsT=w3_mx[b][0][:, rows].bitcast(FP8X4),
+                            lhsT_scale=w3_mx[b][1][:, rows],
+                            rhs=h_mx[b, half][0][:, entries].bitcast(FP8X4),
+                            rhs_scale=h_mx[b, half][1][:, entries],
+                            start=(b == 0 and x == 0),
+                            stop=(b == 1 and x == per_bank - 1),
                         )
                 part = staged[:, width * n0 : width * n0 + W]
                 nc.scalar.activation(out=part, in_=acc[:].rearrange("p x n -> p (x n)"), func=ACT.Silu)
-                dst = out[P * n0 : P * (n0 + per_bank), W * jh + c0 : W * jh + c0 + width]
-                nc.sync.dma_start(out=dst.rearrange("(x p) n -> p x n", p=P), in_=part.rearrange("p (x n) -> p x n", n=width))
+                dst = out[P * n0 : P * (n0 + per_bank), W * half + start : W * half + start + width]
+                nc.sync.dma_start(
+                    out=dst.rearrange("(x p) n -> p x n", p=P), in_=part.rearrange("p (x n) -> p x n", n=width)
+                )
 
-        w1_q[0, 1] = prepare_w1(0, 1, False)
-        load_w3(1, 1, 0)
-        w1_q[1, 1] = prepare_w1(1, 1, False)
-        hidden(0, 0, 1)
-        w3_q = [prepare_w3(0)]
-        hidden(0, 1, 1)
-        w3_q.append(prepare_w3(1))
-        hidden(1, 0, 1)
-        hidden(1, 1, 2)
-        staged = held([P, 4 * W], F32, "gap11")
-        codes_out(0, 0, W, staged[:])
-        last = gaps[1, 0][:].rearrange("p t n -> p (t n)")
-        for half in range(2):
-            codes_out(1, 256 * half, 256, last[:, 1024 * half : 1024 * (half + 1)])
+        w1_mx[0, 1] = prepare_w1(0, 1, late_grouped([P, 4 * W], 0), 0)
+        load_w3(1, 1)
+        w1_mx[1, 1] = prepare_w1(1, 1, late_grouped([P, 4 * W], 1), 0)
+        activate(0, 0)
+        spread_gain()
+        quantise_h(0, 0, 0, 1)
+        w3_mx = [prepare_w3(0)]
+        activate(0, 1)
+        quantise_h(0, 1, 0, 1)
+        w3_mx.append(prepare_w3(1))
+        activate(1, 0)
+        quantise_h(1, 0, 0, 1)
+        activate(1, 1)
+        quantise_h(1, 1, 1, 2)
+        staged_first = held([P, 4 * W], F32, "gap11")
+        defect_codes(0, 0, W, 0, staged_first[:])
+        staged_second = gaps[1, 0][:].rearrange("p t n -> p (t n)")
+        piece_width = W // 2
+        for piece in range(2):
+            staged = staged_second[:, 4 * piece_width * piece : 4 * piece_width * (piece + 1)]
+            defect_codes(1, piece_width * piece, piece_width, 4 + 2 * piece, staged)

@@ -83,11 +83,10 @@ def tile_list_mould_cycle_gap_kernel(
             for t in range(4):
                 nc.sync.dma_start(out=w3_raw[b][:, t, :], in_=rows[b, t])
 
-        def load_plane(queue, plane, rows):
-            for d in range(4):
-                queue.dma_start(
-                    out=plane[32 * d : 32 * d + 4, :].bitcast(I32), in_=rows[4 * d : 4 * d + 4, :].bitcast(I32)
-                )
+        def load_plane(plane, rows):
+            by_row = rows.bitcast(I32).rearrange("(d c) t -> c d t", c=4)
+            for c in range(4):
+                nc.sync.dma_start(out=plane[c:P:32, :].bitcast(I32), in_=by_row[c])
 
         nc.sync.dma_start(list8[:], offs)
         nc.sync.dma_start(list1[:], offs2)
@@ -95,16 +94,21 @@ def tile_list_mould_cycle_gap_kernel(
         tab_scale_rows = tab_scales.bitcast(I32).rearrange("a (g c) t -> c g a t", c=2)
         for c in range(2):
             nc.sync.dma_start(out=tab_scale_window[c:P:8, :].bitcast(I32), in_=tab_scale_rows[c])
+        tab2_scale_rows = tab2_scales[0].bitcast(I32).rearrange("(g c) t -> c g t", c=2)
+        for c in range(2):
+            nc.sync.dma_start(out=tab2_scale_window[c:P:16, :].bitcast(I32), in_=tab2_scale_rows[c])
         tab_windows = [load_table(tab_words[0], "tab_pass0", 0)]
-        load_plane(nc.sync, tab2_scale_window, tab2_scales[0])
         tab_windows.append(load_table(tab_words[1], "tab_pass1", 1))
-        load_w1(0, 0, 2)
-        load_plane(nc.gpsimd, w4_scale_raw, w4_scales[0])
+        load_plane(w4_scale_raw, w4_scales[0])
         gain_view = gain.rearrange("(b m t i) -> b t m i", b=2, t=4, i=4)
         for b in range(2):
-            nc.gpsimd.dma_start(
+            nc.sync.dma_start(
                 out=gain_rows[4 * b : 4 * b + 4, :].rearrange("t (m i) -> t m i", i=4), in_=gain_view[b]
             )
+        load_w1(0, 0, 2)
+        load_w1(1, 0, 3)
+        gain_columns = bank([P, P], "gain_columns", 7)
+        nc.tensor.transpose(gain_columns[:], gain_rows[:], ident[:])
 
         w4_codes = held([P, 2 * H], U8, "w4_codes")
         nc.vector.tensor_copy(
@@ -112,17 +116,18 @@ def tile_list_mould_cycle_gap_kernel(
             w4_raw[:].bitcast(I32).rearrange("p (b m t x) -> p b t m x", b=2, t=4, x=2),
         )
 
-        tab_scale_picked = held([P, S], U8, "tab_scale_picked")
-        tab_planes = held([P, S], U8, "tab_planes")
-        nc.vector.tensor_copy(tab_scale_picked[:], tab_scale_window[:].indirect(list8[:]))
-        nc.vector.tensor_copy(tab_planes[:].bitcast(I32), tab_scale_picked[:].bitcast(I32))
+        scale_picked = held([P, 2 * S], U8, "scale_picked")
+        tab_planes = held([P, 2 * S], U8, "tab_planes")
+        nc.vector.tensor_copy(scale_picked[:, :S], tab_scale_window[:].indirect(list8[:]))
+        nc.vector.tensor_copy(scale_picked[:, S:], tab2_scale_window[:].indirect(list1[:]))
+        nc.vector.tensor_copy(tab_planes[:].bitcast(I32), scale_picked[:].bitcast(I32))
         for a in range(2):
+            columns = slice(0, (2 - a) * S)
             for c in range(2):
                 nc.sync.dma_start(
-                    out=tab_planes[8 * a + 2 + c : P : 32, :].bitcast(I32),
-                    in_=tab_scale_picked[16 + 8 * a + c : P : 32, :].bitcast(I32),
+                    out=tab_planes[8 * a + 2 + c : P : 32, columns].bitcast(I32),
+                    in_=scale_picked[16 + 8 * a + c : P : 32, columns].bitcast(I32),
                 )
-        load_w1(1, 0, 3)
         tab2_window = load_table(tab2_words[0], "tab2", 4)
 
         tab_picked = [held([P, S], U32, "tab_picked%d" % a) for a in range(2)]
@@ -130,8 +135,11 @@ def tile_list_mould_cycle_gap_kernel(
             nc.vector.tensor_copy(tab_picked[a][:], tab_windows[a][:].indirect(list8[:]))
         load_w1(0, 1, 1)
         list1_halves = [list1[:, HALF_COLUMNS * half : HALF_COLUMNS * (half + 1)] for half in range(2)]
-        tab2_planes = [held([P, W], U8, "tab2_plane0")]
-        nc.vector.tensor_copy(tab2_planes[0][:], tab2_scale_window[:].indirect(list1_halves[0]))
+        w4_plane = held([P, H], U8, "w4_plane")
+        nc.vector.tensor_copy(
+            w4_plane[:].bitcast(I32).rearrange("p (b t m) -> p b t m", b=2, t=4),
+            w4_scale_raw[:].bitcast(I32).rearrange("p (b m t) -> p b t m", b=2, t=4),
+        )
 
         def quantise(name, grouped):
             codes = held([P, W], U32, name + "_codes")
@@ -162,27 +170,19 @@ def tile_list_mould_cycle_gap_kernel(
         load_w1(1, 1, 2)
         w1_mx[1, 0] = prepare_w1(1, 0, tenant([P, 4 * W], BF16, "w1_grouped1", 5, GROUPED_BYTES), 2)
         load_w3(0, 3)
-        w4_plane = tenant([P, H], U8, "w4_plane", 5, GROUPED_BYTES)
-        nc.vector.tensor_copy(
-            w4_plane[:].bitcast(I32).rearrange("p (b t m) -> p b t m", b=2, t=4),
-            w4_scale_raw[:].bitcast(I32).rearrange("p (b m t) -> p b t m", b=2, t=4),
-        )
 
         tab2_picked = [held([P, W], U32, "tab2_picked%d" % half) for half in range(2)]
         nc.vector.tensor_copy(tab2_picked[0][:], tab2_window[:].indirect(list1_halves[0]))
-        tab2_planes.append(tenant([P, W], U8, "tab2_plane1", 5, GROUPED_BYTES + H))
-        nc.vector.tensor_copy(tab2_planes[1][:], tab2_scale_window[:].indirect(list1_halves[1]))
         nc.vector.tensor_copy(tab2_picked[1][:], tab2_window[:].indirect(list1_halves[1]))
 
-        gain_columns = held([P, 8], F32, "gain_columns")
+        fills = []
 
-        def spread_gain():
-            turned = bank([P, 5 * W], "gain_turned", 3)
-            nc.tensor.transpose(turned[:, 0:P], gain_rows[:], ident[:])
-            nc.vector.tensor_copy(gain_columns[:], turned[:, 0:8])
+        def next_bank(shape, name):
+            fills.append(name)
+            return bank(shape, name, (len(fills) - 1) % 7)
 
         def difference(b, half, t):
-            acc = bank([P, W], "difference%d%d%d" % (b, half, t), 4 * half + 3 - t)
+            acc = next_bank([P, W], "difference%d%d%d" % (b, half, t))
             entries = slice(W * half, W * (half + 1))
             features = slice(P * t, P * (t + 1))
             for a in range(2):
@@ -202,7 +202,7 @@ def tile_list_mould_cycle_gap_kernel(
                 lhsT=w4_codes[:, 2 * first : 2 * (first + P)].bitcast(FP4X4),
                 lhsT_scale=w4_plane[:, first : first + P],
                 rhs=tab2_picked[half][:].bitcast(FP8X4),
-                rhs_scale=tab2_planes[half][:],
+                rhs_scale=tab_planes[:, S + W * half : S + W * (half + 1)],
                 start=False,
                 stop=True,
             )
@@ -247,11 +247,11 @@ def tile_list_mould_cycle_gap_kernel(
                 )
             h_mx[b, half] = codes, plane
 
-        def defect_codes(half, start, width, first_bank, staged):
+        def defect_codes(half, start, width, staged):
             per_bank = W // width
             entries = slice(start, start + width)
             for n0 in range(0, 4, per_bank):
-                acc = bank([P, per_bank, width], "y%d%d%d" % (half, start, n0), first_bank + n0 // per_bank)
+                acc = next_bank([P, per_bank, width], "y%d%d%d" % (half, start, n0))
                 for b in range(2):
                     for x in range(per_bank):
                         rows = slice(P * (n0 + x), P * (n0 + x + 1))
@@ -275,7 +275,6 @@ def tile_list_mould_cycle_gap_kernel(
         load_w3(1, 1)
         w1_mx[1, 1] = prepare_w1(1, 1, late_grouped([P, 4 * W], 1), 0)
         activate(0, 0)
-        spread_gain()
         quantise_h(0, 0, 0, 1)
         w3_mx = [prepare_w3(0)]
         activate(0, 1)
@@ -286,9 +285,9 @@ def tile_list_mould_cycle_gap_kernel(
         activate(1, 1)
         quantise_h(1, 1, 1, 2)
         staged_first = held([P, 4 * W], F32, "gap11")
-        defect_codes(0, 0, W, 0, staged_first[:])
+        defect_codes(0, 0, W, staged_first[:])
         staged_second = gaps[1, 0][:].rearrange("p t n -> p (t n)")
         piece_width = W // 2
         for piece in range(2):
             staged = staged_second[:, 4 * piece_width * piece : 4 * piece_width * (piece + 1)]
-            defect_codes(1, piece_width * piece, piece_width, 4 + 2 * piece, staged)
+            defect_codes(1, piece_width * piece, piece_width, staged)

@@ -22,6 +22,7 @@ W = 512
 HALF_COLUMNS = W // 16
 BANK_BYTES = 4 * W
 ROOM_BYTES = 9216
+SHARED = (3, 1, 1, 1)
 GROUPED_BYTES = 2 * 4 * W
 
 
@@ -53,15 +54,13 @@ def tile_list_mould_cycle_gap_kernel(
         tab2_scale_window = held([P, T], U8, "tab2_scale_window")
         w4_raw = held([P, 2 * H], U8, "w4_raw")
         w4_scale_raw = held([P, H], U8, "w4_scale_raw")
-        gain_rows = held([P, P], F32, "gain_rows")
         ident = held([P, P], F32, "ident")
         w1_raw = {}
         w3_raw = {}
 
-        nc.vector.memset(tab_scale_window[:].bitcast(I32), 0)
+        nc.gpsimd.memset(tab_scale_window[:].bitcast(I32), 0)
         nc.vector.memset(tab2_scale_window[:].bitcast(I32), 0)
         nc.gpsimd.memset(w4_scale_raw[:].bitcast(I32), 0)
-        nc.vector.memset(gain_rows[:], 0.0)
         make_identity(nc, ident[:])
         zero_bias = held([P, 1], F32, "zero_bias")
         nc.gpsimd.memset(zero_bias[:], 0.0)
@@ -83,32 +82,31 @@ def tile_list_mould_cycle_gap_kernel(
             for t in range(4):
                 nc.sync.dma_start(out=w3_raw[b][:, t, :], in_=rows[b, t])
 
-        def load_plane(plane, rows):
-            by_row = rows.bitcast(I32).rearrange("(d c) t -> c d t", c=4)
-            for c in range(4):
-                nc.sync.dma_start(out=plane[c:P:32, :].bitcast(I32), in_=by_row[c])
+        def load_w4_scale_rows(c):
+            rows = w4_scales[0].bitcast(I32).rearrange("(d c) t -> c d t", c=4)
+            nc.sync.dma_start(out=w4_scale_raw[c:P:32, :].bitcast(I32), in_=rows[c])
+
+        def load_gain(b, gain_rows):
+            rows = gain.rearrange("(b m t i) -> b t m i", b=2, t=4, i=4)
+            nc.sync.dma_start(out=gain_rows[4 * b : 4 * b + 4, :].rearrange("t (m i) -> t m i", i=4), in_=rows[b])
 
         nc.sync.dma_start(list8[:], offs)
-        nc.sync.dma_start(list1[:], offs2)
-        nc.sync.dma_start(out=w4_raw[:].bitcast(I32), in_=w4_words[0].bitcast(I32))
         tab_scale_rows = tab_scales.bitcast(I32).rearrange("a (g c) t -> c g a t", c=2)
         for c in range(2):
             nc.sync.dma_start(out=tab_scale_window[c:P:8, :].bitcast(I32), in_=tab_scale_rows[c])
+        nc.sync.dma_start(list1[:], offs2)
         tab2_scale_rows = tab2_scales[0].bitcast(I32).rearrange("(g c) t -> c g t", c=2)
         for c in range(2):
             nc.sync.dma_start(out=tab2_scale_window[c:P:16, :].bitcast(I32), in_=tab2_scale_rows[c])
         tab_windows = [load_table(tab_words[0], "tab_pass0", 0)]
-        tab_windows.append(load_table(tab_words[1], "tab_pass1", 1))
-        load_plane(w4_scale_raw, w4_scales[0])
-        gain_view = gain.rearrange("(b m t i) -> b t m i", b=2, t=4, i=4)
-        for b in range(2):
-            nc.sync.dma_start(
-                out=gain_rows[4 * b : 4 * b + 4, :].rearrange("t (m i) -> t m i", i=4), in_=gain_view[b]
-            )
         load_w1(0, 0, 2)
+        load_w4_scale_rows(0)
+        load_w4_scale_rows(1)
+        tab_windows.append(load_table(tab_words[1], "tab_pass1", 1))
+        load_w4_scale_rows(2)
+        load_w4_scale_rows(3)
+        nc.sync.dma_start(out=w4_raw[:].bitcast(I32), in_=w4_words[0].bitcast(I32))
         load_w1(1, 0, 3)
-        gain_columns = bank([P, P], "gain_columns", 7)
-        nc.tensor.transpose(gain_columns[:], gain_rows[:], ident[:])
 
         w4_codes = held([P, 2 * H], U8, "w4_codes")
         nc.vector.tensor_copy(
@@ -116,24 +114,34 @@ def tile_list_mould_cycle_gap_kernel(
             w4_raw[:].bitcast(I32).rearrange("p (b m t x) -> p b t m x", b=2, t=4, x=2),
         )
 
-        scale_picked = held([P, 2 * S], U8, "scale_picked")
-        tab_planes = held([P, 2 * S], U8, "tab_planes")
+        scale_picked = tenant([P, 2 * S], U8, "scale_picked", 4, 4 * T - S // 2)
+        tab_planes = [held([P, (2 - a) * S], U8, "tab_planes%d" % a) for a in range(2)]
         nc.vector.tensor_copy(scale_picked[:, :S], tab_scale_window[:].indirect(list8[:]))
         nc.vector.tensor_copy(scale_picked[:, S:], tab2_scale_window[:].indirect(list1[:]))
-        nc.vector.tensor_copy(tab_planes[:].bitcast(I32), scale_picked[:].bitcast(I32))
         for a in range(2):
-            columns = slice(0, (2 - a) * S)
+            nc.vector.tensor_copy(tab_planes[a][:].bitcast(I32), scale_picked[:, : (2 - a) * S].bitcast(I32))
+
+        def move_odd_rows(a):
             for c in range(2):
                 nc.sync.dma_start(
-                    out=tab_planes[8 * a + 2 + c : P : 32, columns].bitcast(I32),
-                    in_=scale_picked[16 + 8 * a + c : P : 32, columns].bitcast(I32),
+                    out=tab_planes[a][8 * a + 2 + c : P : 32, :].bitcast(I32),
+                    in_=tab_planes[a][16 + 8 * a + c : P : 32, :].bitcast(I32),
                 )
+
+        move_odd_rows(0)
         tab2_window = load_table(tab2_words[0], "tab2", 4)
+        move_odd_rows(1)
 
         tab_picked = [held([P, S], U32, "tab_picked%d" % a) for a in range(2)]
         for a in range(2):
             nc.vector.tensor_copy(tab_picked[a][:], tab_windows[a][:].indirect(list8[:]))
-        load_w1(0, 1, 1)
+        load_w1(0, 1, 5)
+        gain_rows = tenant([P, P], F32, "gain_rows", 4, 4 * T)
+        nc.vector.memset(gain_rows[:], 0.0)
+        for b in range(2):
+            load_gain(b, gain_rows)
+        gain_columns = bank([P, P], "gain_columns", 7)
+        nc.tensor.transpose(gain_columns[:], gain_rows[:], ident[:])
         list1_halves = [list1[:, HALF_COLUMNS * half : HALF_COLUMNS * (half + 1)] for half in range(2)]
         w4_plane = held([P, H], U8, "w4_plane")
         nc.vector.tensor_copy(
@@ -141,11 +149,19 @@ def tile_list_mould_cycle_gap_kernel(
             w4_scale_raw[:].bitcast(I32).rearrange("p (b m t) -> p b t m", b=2, t=4),
         )
 
-        def quantise(name, grouped):
-            codes = held([P, W], U32, name + "_codes")
+        def quantise(name, grouped, codes=None):
+            if codes is None:
+                codes = held([P, W], U32, name + "_codes")
             plane = held([P, W], U8, name + "_plane")
-            nc.vector.quantize_mx(out=codes[:].bitcast(FP8X4), scales=plane[:], in_=grouped[:])
+            nc.vector.quantize_mx(out=codes[:].bitcast(FP8X4), scales=plane[:], in_=grouped)
             return codes, plane
+
+        def round_w1_on_gpsimd(a, b, grouped):
+            src = w1_raw[a, b][:].rearrange("p j (m t i) -> p t m i j", t=4, i=4)
+            dst = grouped[:].rearrange("p (t m i j) -> p t m i j", t=4, i=4, j=4)
+            for t in range(4):
+                nc.gpsimd.tensor_scalar(dst[:, t], src[:, t], -1.0, 0.0, ALU.mult, ALU.add)
+            return quantise("w1_%d%d" % (a, b), grouped[:])
 
         def prepare_w1(a, b, grouped, tiles_on_scalar):
             src = w1_raw[a, b][:].rearrange("p j (m t i) -> p t m j i", t=4, i=4)
@@ -155,23 +171,33 @@ def tile_list_mould_cycle_gap_kernel(
                     nc.scalar.activation(out=dst[:, t], in_=src[:, t], func=ACT.Copy, scale=-1.0)
                 else:
                     nc.vector.tensor_scalar(dst[:, t], src[:, t], -1.0, None, ALU.mult)
-            return quantise("w1_%d%d" % (a, b), grouped)
+            return quantise("w1_%d%d" % (a, b), grouped[:])
 
-        def prepare_w3(b):
-            grouped = late_grouped([P, 4 * N], 1)
-            nc.vector.tensor_copy(
-                grouped[:].rearrange("p (c i t) -> p c t i", i=4, t=4),
-                w3_raw[b][:].rearrange("p t (c i) -> p c t i", i=4),
-            )
-            return quantise("w3_%d" % b, grouped)
+        def round_w3(b):
+            grouped = held([P, N, 4], BF16, "w3_grouped%d" % b)
+            for n0 in range(0, N, P):
+                nc.gpsimd.tensor_scalar(
+                    grouped[:, n0 : n0 + P, :],
+                    w3_raw[b][:, :, n0 : n0 + P].rearrange("p t n -> p n t"),
+                    1.0,
+                    0.0,
+                    ALU.mult,
+                    ALU.add,
+                )
+            return grouped
+
+        def quantise_w3(b, grouped):
+            codes = tenant([P, W], U32, "w3_codes%d" % b, 6, GROUPED_BYTES * b)
+            return quantise("w3_%d" % b, grouped[:].rearrange("p n t -> p (n t)"), codes)
 
         w1_mx = {}
-        w1_mx[0, 0] = prepare_w1(0, 0, tenant([P, 4 * W], BF16, "w1_grouped0", 5), 4)
+        w1_mx[0, 0] = prepare_w1(0, 0, tenant([P, 4 * W], BF16, "w1_grouped0", 8), 4)
         load_w1(1, 1, 2)
-        w1_mx[1, 0] = prepare_w1(1, 0, tenant([P, 4 * W], BF16, "w1_grouped1", 5, GROUPED_BYTES), 2)
-        load_w3(0, 3)
+        w1_mx[1, 0] = prepare_w1(1, 0, tenant([P, 4 * W], BF16, "w1_grouped1", 8, GROUPED_BYTES), 4)
+        load_w3(0, 1)
+        load_w3(1, 3)
 
-        tab2_picked = [held([P, W], U32, "tab2_picked%d" % half) for half in range(2)]
+        tab2_picked = [held([P, W], U32, "tab2_picked0"), tenant([P, W], U32, "tab2_picked1", 8, GROUPED_BYTES)]
         nc.vector.tensor_copy(tab2_picked[0][:], tab2_window[:].indirect(list1_halves[0]))
         nc.vector.tensor_copy(tab2_picked[1][:], tab2_window[:].indirect(list1_halves[1]))
 
@@ -185,59 +211,67 @@ def tile_list_mould_cycle_gap_kernel(
             acc = next_bank([P, W], "difference%d%d%d" % (b, half, t))
             entries = slice(W * half, W * (half + 1))
             features = slice(P * t, P * (t + 1))
-            for a in range(2):
+            first = W * b + P * t
+
+            def w1_pass(a):
                 codes, plane = w1_mx[a, b]
                 nc.tensor.matmul_mx(
                     out=acc[:],
                     lhsT=codes[:, features].bitcast(FP8X4),
                     lhsT_scale=plane[:, features],
                     rhs=tab_picked[a][:, entries].bitcast(FP8X4),
-                    rhs_scale=tab_planes[8 * a : P, entries],
+                    rhs_scale=tab_planes[a][8 * a : P, entries],
                     start=(a == 0),
-                    stop=False,
+                    stop=(a == 1),
                 )
-            first = W * b + P * t
+
+            w1_pass(0)
             nc.tensor.matmul_mx(
                 out=acc[:],
                 lhsT=w4_codes[:, 2 * first : 2 * (first + P)].bitcast(FP4X4),
                 lhsT_scale=w4_plane[:, first : first + P],
                 rhs=tab2_picked[half][:].bitcast(FP8X4),
-                rhs_scale=tab_planes[:, S + W * half : S + W * (half + 1)],
+                rhs_scale=tab_planes[0][:, S + W * half : S + W * (half + 1)],
                 start=False,
-                stop=True,
+                stop=False,
             )
+            w1_pass(1)
             return acc
 
         gaps = {}
         acts = {}
         h_mx = {}
 
-        def activate(b, half):
+        def activate(b, half, shared):
             gap = held([P, 4, W], F32, "gap%d%d" % (b, half))
+            act = ring.tile([P, 4, W], F32, name="act", align_bytes=64)
             for t in range(4):
-                nc.scalar.activation(out=gap[:, t, :], in_=difference(b, half, t)[:], func=ACT.Abs)
-            act = ring.tile([P, 2, W, 2], F32, name="act", align_bytes=64)
+                acc = difference(b, half, t)
+                if t < shared:
+                    nc.scalar.activation(
+                        out=gap[:, t, :], in_=acc[:], func=ACT.Gelu_apprx_tanh, bias=zero_bias[:], scale=-1.0
+                    )
+                    nc.vector.scalar_tensor_tensor(act[:, t, :], acc[:], 0.0, gap[:, t, :], ALU.max, ALU.add)
+                else:
+                    nc.scalar.activation(out=gap[:, t, :], in_=acc[:], func=ACT.Abs)
             nc.scalar.activation(
-                out=act[:],
-                in_=gap[:].rearrange("p (u e) n -> p u n e", e=2),
-                func=ACT.Gelu_apprx_tanh,
-                bias=zero_bias[:],
+                out=act[:, shared:, :], in_=gap[:, shared:, :], func=ACT.Gelu_apprx_tanh, bias=zero_bias[:]
             )
             gaps[b, half] = gap
             acts[b, half] = act
 
-        def quantise_h(b, half, side, pieces):
-            grouped = late_grouped([P, W, 4], side)
+        def quantise_h(b, half, pieces):
+            grouped = tenant([P, W, 4], BF16, "h_grouped%d%d" % (b, half), 6 + b, GROUPED_BYTES * half)
             codes = held([P, W], U32, "h_codes%d%d" % (b, half))
             plane = held([P, W], U8, "h_plane%d%d" % (b, half))
             width = W // pieces
-            gains = gain_columns[:, 4 * b : 4 * b + 4].rearrange("p (u e) -> p u e", e=2)
+            gains = gain_columns[:, 4 * b : 4 * b + 4]
             for piece in range(pieces):
                 n = slice(width * piece, width * (piece + 1))
                 nc.vector.tensor_tensor(
-                    grouped[:, n, :].rearrange("p n (u e) -> p n u e", e=2),
-                    acts[b, half][:, :, n, :].rearrange("p u n e -> p n u e"),
-                    gains.unsqueeze(1).to_broadcast([P, width, 2, 2]),
+                    grouped[:, n, :].rearrange("p (c i) t -> p c t i", i=2),
+                    acts[b, half][:, :, n].rearrange("p t (c i) -> p c t i", i=2),
+                    gains.unsqueeze(1).unsqueeze(3).to_broadcast([P, width // 2, 4, 2]),
                     ALU.mult,
                 )
                 nc.vector.quantize_mx(
@@ -271,19 +305,19 @@ def tile_list_mould_cycle_gap_kernel(
                     out=dst.rearrange("(x p) n -> p x n", p=P), in_=part.rearrange("p (x n) -> p x n", n=width)
                 )
 
-        w1_mx[0, 1] = prepare_w1(0, 1, late_grouped([P, 4 * W], 0), 0)
-        load_w3(1, 1)
-        w1_mx[1, 1] = prepare_w1(1, 1, late_grouped([P, 4 * W], 1), 0)
-        activate(0, 0)
-        quantise_h(0, 0, 0, 1)
-        w3_mx = [prepare_w3(0)]
-        activate(0, 1)
-        quantise_h(0, 1, 0, 1)
-        w3_mx.append(prepare_w3(1))
-        activate(1, 0)
-        quantise_h(1, 0, 0, 1)
-        activate(1, 1)
-        quantise_h(1, 1, 1, 2)
+        w1_mx[0, 1] = round_w1_on_gpsimd(0, 1, tenant([P, 4 * W], BF16, "w1_grouped2", 6))
+        w1_mx[1, 1] = round_w1_on_gpsimd(1, 1, tenant([P, 4 * W], BF16, "w1_grouped3", 6, GROUPED_BYTES))
+        w3_grouped = [round_w3(b) for b in range(2)]
+        activate(0, 0, SHARED[0])
+        quantise_h(0, 0, 1)
+        w3_mx = [quantise_w3(0, w3_grouped[0])]
+        activate(0, 1, SHARED[1])
+        quantise_h(0, 1, 1)
+        w3_mx.append(quantise_w3(1, w3_grouped[1]))
+        activate(1, 0, SHARED[2])
+        quantise_h(1, 0, 1)
+        activate(1, 1, SHARED[3])
+        quantise_h(1, 1, 2)
         staged_first = held([P, 4 * W], F32, "gap11")
         defect_codes(0, 0, W, staged_first[:])
         staged_second = gaps[1, 0][:].rearrange("p t n -> p (t n)")

@@ -22,7 +22,8 @@ W = 512
 HALF_COLUMNS = W // 16
 BANK_BYTES = 4 * W
 ROOM_BYTES = 9216
-SHARED = (3, 1, 1, 1)
+WHOLE = ((0, W),)
+LAST_PIECES = ((0, 256), (256, 128), (384, 128))
 GROUPED_BYTES = 2 * 4 * W
 
 
@@ -98,15 +99,13 @@ def tile_list_mould_cycle_gap_kernel(
         tab2_scale_rows = tab2_scales[0].bitcast(I32).rearrange("(g c) t -> c g t", c=2)
         for c in range(2):
             nc.sync.dma_start(out=tab2_scale_window[c:P:16, :].bitcast(I32), in_=tab2_scale_rows[c])
-        tab_windows = [load_table(tab_words[0], "tab_pass0", 0)]
         load_w1(0, 0, 2)
-        load_w4_scale_rows(0)
-        load_w4_scale_rows(1)
-        tab_windows.append(load_table(tab_words[1], "tab_pass1", 1))
-        load_w4_scale_rows(2)
-        load_w4_scale_rows(3)
-        nc.sync.dma_start(out=w4_raw[:].bitcast(I32), in_=w4_words[0].bitcast(I32))
+        tab_windows = [load_table(tab_words[0], "tab_pass0", 0)]
+        for c in range(4):
+            load_w4_scale_rows(c)
         load_w1(1, 0, 3)
+        nc.sync.dma_start(out=w4_raw[:].bitcast(I32), in_=w4_words[0].bitcast(I32))
+        tab_windows.append(load_table(tab_words[1], "tab_pass1", 1))
 
         w4_codes = held([P, 2 * H], U8, "w4_codes")
         nc.vector.tensor_copy(
@@ -115,33 +114,35 @@ def tile_list_mould_cycle_gap_kernel(
         )
 
         scale_picked = tenant([P, 2 * S], U8, "scale_picked", 4, 4 * T - S // 2)
-        tab_planes = [held([P, (2 - a) * S], U8, "tab_planes%d" % a) for a in range(2)]
+        tab_planes = held([P, 2 * S], U8, "tab_planes")
         nc.vector.tensor_copy(scale_picked[:, :S], tab_scale_window[:].indirect(list8[:]))
         nc.vector.tensor_copy(scale_picked[:, S:], tab2_scale_window[:].indirect(list1[:]))
-        for a in range(2):
-            nc.vector.tensor_copy(tab_planes[a][:].bitcast(I32), scale_picked[:, : (2 - a) * S].bitcast(I32))
+        nc.vector.tensor_copy(tab_planes[:].bitcast(I32), scale_picked[:].bitcast(I32))
 
         def move_odd_rows(a):
+            columns = slice(0, (2 - a) * S)
             for c in range(2):
                 nc.sync.dma_start(
-                    out=tab_planes[a][8 * a + 2 + c : P : 32, :].bitcast(I32),
-                    in_=tab_planes[a][16 + 8 * a + c : P : 32, :].bitcast(I32),
+                    out=tab_planes[8 * a + 2 + c : P : 32, columns].bitcast(I32),
+                    in_=tab_planes[16 + 8 * a + c : P : 32, columns].bitcast(I32),
                 )
 
         move_odd_rows(0)
-        tab2_window = load_table(tab2_words[0], "tab2", 4)
         move_odd_rows(1)
+        tab2_window = load_table(tab2_words[0], "tab2", 4)
 
-        tab_picked = [held([P, S], U32, "tab_picked%d" % a) for a in range(2)]
-        for a in range(2):
-            nc.vector.tensor_copy(tab_picked[a][:], tab_windows[a][:].indirect(list8[:]))
+        list8_halves = [list8[:, HALF_COLUMNS * half : HALF_COLUMNS * (half + 1)] for half in range(2)]
+        pass0_picked = held([P, S], U32, "pass0_picked")
+        nc.vector.tensor_copy(pass0_picked[:], tab_windows[0][:].indirect(list8[:]))
+        tab_picked = {(0, half): pass0_picked[:, W * half : W * (half + 1)] for half in range(2)}
+        pass1_picked = [held([P, W], U32, "pass1_picked0")]
+        nc.vector.tensor_copy(pass1_picked[0][:], tab_windows[1][:].indirect(list8_halves[0]))
+        tab_picked[1, 0] = pass1_picked[0][:]
         load_w1(0, 1, 5)
         gain_rows = tenant([P, P], F32, "gain_rows", 4, 4 * T)
         nc.vector.memset(gain_rows[:], 0.0)
         for b in range(2):
             load_gain(b, gain_rows)
-        gain_columns = bank([P, P], "gain_columns", 7)
-        nc.tensor.transpose(gain_columns[:], gain_rows[:], ident[:])
         list1_halves = [list1[:, HALF_COLUMNS * half : HALF_COLUMNS * (half + 1)] for half in range(2)]
         w4_plane = held([P, H], U8, "w4_plane")
         nc.vector.tensor_copy(
@@ -156,13 +157,6 @@ def tile_list_mould_cycle_gap_kernel(
             nc.vector.quantize_mx(out=codes[:].bitcast(FP8X4), scales=plane[:], in_=grouped)
             return codes, plane
 
-        def round_w1_on_gpsimd(a, b, grouped):
-            src = w1_raw[a, b][:].rearrange("p j (m t i) -> p t m i j", t=4, i=4)
-            dst = grouped[:].rearrange("p (t m i j) -> p t m i j", t=4, i=4, j=4)
-            for t in range(4):
-                nc.gpsimd.tensor_scalar(dst[:, t], src[:, t], -1.0, 0.0, ALU.mult, ALU.add)
-            return quantise("w1_%d%d" % (a, b), grouped[:])
-
         def prepare_w1(a, b, grouped, tiles_on_scalar):
             src = w1_raw[a, b][:].rearrange("p j (m t i) -> p t m j i", t=4, i=4)
             dst = grouped[:].rearrange("p (t m i j) -> p t m j i", t=4, i=4, j=4)
@@ -173,42 +167,30 @@ def tile_list_mould_cycle_gap_kernel(
                     nc.vector.tensor_scalar(dst[:, t], src[:, t], -1.0, None, ALU.mult)
             return quantise("w1_%d%d" % (a, b), grouped[:])
 
-        def round_w3(b):
-            grouped = held([P, N, 4], BF16, "w3_grouped%d" % b)
-            for n0 in range(0, N, P):
-                nc.gpsimd.tensor_scalar(
-                    grouped[:, n0 : n0 + P, :],
-                    w3_raw[b][:, :, n0 : n0 + P].rearrange("p t n -> p n t"),
-                    1.0,
-                    0.0,
-                    ALU.mult,
-                    ALU.add,
-                )
-            return grouped
-
-        def quantise_w3(b, grouped):
-            codes = tenant([P, W], U32, "w3_codes%d" % b, 6, GROUPED_BYTES * b)
-            return quantise("w3_%d" % b, grouped[:].rearrange("p n t -> p (n t)"), codes)
+        def prepare_w3(b):
+            grouped = held([P, 4 * N], BF16, "w3_grouped%d" % b)
+            nc.vector.tensor_copy(
+                grouped[:].rearrange("p (c i t) -> p c t i", i=4, t=4),
+                w3_raw[b][:].rearrange("p t (c i) -> p c t i", i=4),
+            )
+            return quantise("w3_%d" % b, grouped[:])
 
         w1_mx = {}
         w1_mx[0, 0] = prepare_w1(0, 0, tenant([P, 4 * W], BF16, "w1_grouped0", 8), 4)
         load_w1(1, 1, 2)
         w1_mx[1, 0] = prepare_w1(1, 0, tenant([P, 4 * W], BF16, "w1_grouped1", 8, GROUPED_BYTES), 4)
-        load_w3(0, 1)
-        load_w3(1, 3)
+        load_w3(0, 3)
+        load_w3(1, 8)
 
-        tab2_picked = [held([P, W], U32, "tab2_picked0"), tenant([P, W], U32, "tab2_picked1", 8, GROUPED_BYTES)]
+        tab2_picked = [held([P, W], U32, "tab2_picked%d" % half) for half in range(2)]
         nc.vector.tensor_copy(tab2_picked[0][:], tab2_window[:].indirect(list1_halves[0]))
         nc.vector.tensor_copy(tab2_picked[1][:], tab2_window[:].indirect(list1_halves[1]))
+        pass1_picked.append(tenant([P, W], U32, "pass1_picked1", 4))
+        nc.vector.tensor_copy(pass1_picked[1][:], tab_windows[1][:].indirect(list8_halves[1]))
+        tab_picked[1, 1] = pass1_picked[1][:]
 
-        fills = []
-
-        def next_bank(shape, name):
-            fills.append(name)
-            return bank(shape, name, (len(fills) - 1) % 7)
-
-        def difference(b, half, t):
-            acc = next_bank([P, W], "difference%d%d%d" % (b, half, t))
+        def difference_passes(b, half, t):
+            acc = bank([P, W], "difference%d%d%d" % (b, half, t), t)
             entries = slice(W * half, W * (half + 1))
             features = slice(P * t, P * (t + 1))
             first = W * b + P * t
@@ -219,43 +201,46 @@ def tile_list_mould_cycle_gap_kernel(
                     out=acc[:],
                     lhsT=codes[:, features].bitcast(FP8X4),
                     lhsT_scale=plane[:, features],
-                    rhs=tab_picked[a][:, entries].bitcast(FP8X4),
-                    rhs_scale=tab_planes[a][8 * a : P, entries],
+                    rhs=tab_picked[a, half].bitcast(FP8X4),
+                    rhs_scale=tab_planes[8 * a : P, entries],
                     start=(a == 0),
-                    stop=(a == 1),
+                    stop=False,
                 )
 
-            w1_pass(0)
-            nc.tensor.matmul_mx(
-                out=acc[:],
-                lhsT=w4_codes[:, 2 * first : 2 * (first + P)].bitcast(FP4X4),
-                lhsT_scale=w4_plane[:, first : first + P],
-                rhs=tab2_picked[half][:].bitcast(FP8X4),
-                rhs_scale=tab_planes[0][:, S + W * half : S + W * (half + 1)],
-                start=False,
-                stop=False,
-            )
-            w1_pass(1)
-            return acc
+            def w4_pass():
+                nc.tensor.matmul_mx(
+                    out=acc[:],
+                    lhsT=w4_codes[:, 2 * first : 2 * (first + P)].bitcast(FP4X4),
+                    lhsT_scale=w4_plane[:, first : first + P],
+                    rhs=tab2_picked[half][:].bitcast(FP8X4),
+                    rhs_scale=tab_planes[:, S + W * half : S + W * (half + 1)],
+                    start=False,
+                    stop=True,
+                )
 
+            return acc, [lambda: w1_pass(0), lambda: w1_pass(1), w4_pass]
+
+        y_banks = [4, 5, 6, 0, 1, 2, 3, 4]
         gaps = {}
         acts = {}
         h_mx = {}
 
-        def activate(b, half, shared):
+        def activate(b, half, early=0):
             gap = held([P, 4, W], F32, "gap%d%d" % (b, half))
-            act = ring.tile([P, 4, W], F32, name="act", align_bytes=64)
-            for t in range(4):
-                acc = difference(b, half, t)
-                if t < shared:
-                    nc.scalar.activation(
-                        out=gap[:, t, :], in_=acc[:], func=ACT.Gelu_apprx_tanh, bias=zero_bias[:], scale=-1.0
-                    )
-                    nc.vector.scalar_tensor_tensor(act[:, t, :], acc[:], 0.0, gap[:, t, :], ALU.max, ALU.add)
-                else:
-                    nc.scalar.activation(out=gap[:, t, :], in_=acc[:], func=ACT.Abs)
+            groups = [difference_passes(b, half, t) for t in range(4)]
+            for step in range(early):
+                for acc, passes in groups:
+                    passes[step]()
+            for t, (acc, passes) in enumerate(groups):
+                for one_pass in passes[early:]:
+                    one_pass()
+                nc.scalar.activation(out=gap[:, t, :], in_=acc[:], func=ACT.Abs)
+            act = ring.tile([P, 2, W, 2], F32, name="act", align_bytes=64)
             nc.scalar.activation(
-                out=act[:, shared:, :], in_=gap[:, shared:, :], func=ACT.Gelu_apprx_tanh, bias=zero_bias[:]
+                out=act[:],
+                in_=gap[:].rearrange("p (u e) n -> p u n e", e=2),
+                func=ACT.Gelu_apprx_tanh,
+                bias=zero_bias[:],
             )
             gaps[b, half] = gap
             acts[b, half] = act
@@ -264,14 +249,13 @@ def tile_list_mould_cycle_gap_kernel(
             grouped = tenant([P, W, 4], BF16, "h_grouped%d%d" % (b, half), 6 + b, GROUPED_BYTES * half)
             codes = held([P, W], U32, "h_codes%d%d" % (b, half))
             plane = held([P, W], U8, "h_plane%d%d" % (b, half))
-            width = W // pieces
-            gains = gain_columns[:, 4 * b : 4 * b + 4]
-            for piece in range(pieces):
-                n = slice(width * piece, width * (piece + 1))
+            gains = gain_columns[:, 4 * b : 4 * b + 4].rearrange("p (u e) -> p u e", e=2)
+            for start, width in pieces:
+                n = slice(start, start + width)
                 nc.vector.tensor_tensor(
-                    grouped[:, n, :].rearrange("p (c i) t -> p c t i", i=2),
-                    acts[b, half][:, :, n].rearrange("p t (c i) -> p c t i", i=2),
-                    gains.unsqueeze(1).unsqueeze(3).to_broadcast([P, width // 2, 4, 2]),
+                    grouped[:, n, :].rearrange("p n (u e) -> p n u e", e=2),
+                    acts[b, half][:, :, n, :].rearrange("p u n e -> p n u e"),
+                    gains.unsqueeze(1).to_broadcast([P, width, 2, 2]),
                     ALU.mult,
                 )
                 nc.vector.quantize_mx(
@@ -285,7 +269,7 @@ def tile_list_mould_cycle_gap_kernel(
             per_bank = W // width
             entries = slice(start, start + width)
             for n0 in range(0, 4, per_bank):
-                acc = next_bank([P, per_bank, width], "y%d%d%d" % (half, start, n0))
+                acc = bank([P, per_bank, width], "y%d%d%d" % (half, start, n0), y_banks.pop(0))
                 for b in range(2):
                     for x in range(per_bank):
                         rows = slice(P * (n0 + x), P * (n0 + x + 1))
@@ -305,23 +289,22 @@ def tile_list_mould_cycle_gap_kernel(
                     out=dst.rearrange("(x p) n -> p x n", p=P), in_=part.rearrange("p (x n) -> p x n", n=width)
                 )
 
-        w1_mx[0, 1] = round_w1_on_gpsimd(0, 1, tenant([P, 4 * W], BF16, "w1_grouped2", 6))
-        w1_mx[1, 1] = round_w1_on_gpsimd(1, 1, tenant([P, 4 * W], BF16, "w1_grouped3", 6, GROUPED_BYTES))
-        w3_grouped = [round_w3(b) for b in range(2)]
-        activate(0, 0, SHARED[0])
-        quantise_h(0, 0, 1)
-        w3_mx = [quantise_w3(0, w3_grouped[0])]
-        activate(0, 1, SHARED[1])
-        quantise_h(0, 1, 1)
-        w3_mx.append(quantise_w3(1, w3_grouped[1]))
-        activate(1, 0, SHARED[2])
-        quantise_h(1, 0, 1)
-        activate(1, 1, SHARED[3])
-        quantise_h(1, 1, 2)
+        w1_mx[0, 1] = prepare_w1(0, 1, tenant([P, 4 * W], BF16, "w1_grouped2", 6, GROUPED_BYTES), 0)
+        w1_mx[1, 1] = prepare_w1(1, 1, tenant([P, 4 * W], BF16, "w1_grouped3", 6), 0)
+        activate(0, 0, 2)
+        gain_columns = bank([P, P], "gain_columns", 7)
+        nc.tensor.transpose(gain_columns[:], gain_rows[:], ident[:])
+        quantise_h(0, 0, WHOLE)
+        w3_mx = [prepare_w3(0)]
+        activate(0, 1)
+        quantise_h(0, 1, WHOLE)
+        w3_mx.append(prepare_w3(1))
+        activate(1, 0)
+        quantise_h(1, 0, WHOLE)
+        activate(1, 1)
+        quantise_h(1, 1, LAST_PIECES)
         staged_first = held([P, 4 * W], F32, "gap11")
         defect_codes(0, 0, W, staged_first[:])
         staged_second = gaps[1, 0][:].rearrange("p t n -> p (t n)")
-        piece_width = W // 2
-        for piece in range(2):
-            staged = staged_second[:, 4 * piece_width * piece : 4 * piece_width * (piece + 1)]
-            defect_codes(1, piece_width * piece, piece_width, staged)
+        for start, width in LAST_PIECES:
+            defect_codes(1, start, width, staged_second[:, 4 * start : 4 * (start + width)])

@@ -23,7 +23,7 @@ HALF_COLUMNS = W // 16
 BANK_BYTES = 4 * W
 ROOM_BYTES = 9216
 WHOLE = ((0, W),)
-LAST_PIECES = ((0, 256), (256, 128), (384, 128))
+LAST_PIECES = ((0, 256), (256, 256))
 GROUPED_BYTES = 2 * 4 * W
 
 
@@ -131,18 +131,10 @@ def tile_list_mould_cycle_gap_kernel(
         move_odd_rows(1)
         tab2_window = load_table(tab2_words[0], "tab2", 4)
 
-        list8_halves = [list8[:, HALF_COLUMNS * half : HALF_COLUMNS * (half + 1)] for half in range(2)]
-        pass0_picked = held([P, S], U32, "pass0_picked")
-        nc.vector.tensor_copy(pass0_picked[:], tab_windows[0][:].indirect(list8[:]))
-        tab_picked = {(0, half): pass0_picked[:, W * half : W * (half + 1)] for half in range(2)}
-        pass1_picked = [held([P, W], U32, "pass1_picked0")]
-        nc.vector.tensor_copy(pass1_picked[0][:], tab_windows[1][:].indirect(list8_halves[0]))
-        tab_picked[1, 0] = pass1_picked[0][:]
+        tab_picked = [held([P, S], U32, "tab_picked%d" % a) for a in range(2)]
+        for a in range(2):
+            nc.vector.tensor_copy(tab_picked[a][:], tab_windows[a][:].indirect(list8[:]))
         load_w1(0, 1, 5)
-        gain_rows = tenant([P, P], F32, "gain_rows", 4, 4 * T)
-        nc.vector.memset(gain_rows[:], 0.0)
-        for b in range(2):
-            load_gain(b, gain_rows)
         list1_halves = [list1[:, HALF_COLUMNS * half : HALF_COLUMNS * (half + 1)] for half in range(2)]
         w4_plane = held([P, H], U8, "w4_plane")
         nc.vector.tensor_copy(
@@ -167,17 +159,21 @@ def tile_list_mould_cycle_gap_kernel(
                     nc.vector.tensor_scalar(dst[:, t], src[:, t], -1.0, None, ALU.mult)
             return quantise("w1_%d%d" % (a, b), grouped[:])
 
-        def prepare_w3(b):
-            grouped = held([P, 4 * N], BF16, "w3_grouped%d" % b)
+        def round_w3(b):
+            grouped = tenant([P, 4 * N], BF16, "w3_grouped%d" % b, 1, GROUPED_BYTES * b)
             nc.vector.tensor_copy(
                 grouped[:].rearrange("p (c i t) -> p c t i", i=4, t=4),
                 w3_raw[b][:].rearrange("p t (c i) -> p c t i", i=4),
             )
-            return quantise("w3_%d" % b, grouped[:])
+            return grouped
 
         w1_mx = {}
         w1_mx[0, 0] = prepare_w1(0, 0, tenant([P, 4 * W], BF16, "w1_grouped0", 8), 4)
         load_w1(1, 1, 2)
+        gain_rows = tenant([P, P], F32, "gain_rows", 0)
+        nc.vector.memset(gain_rows[:], 0.0)
+        for b in range(2):
+            load_gain(b, gain_rows)
         w1_mx[1, 0] = prepare_w1(1, 0, tenant([P, 4 * W], BF16, "w1_grouped1", 8, GROUPED_BYTES), 4)
         load_w3(0, 3)
         load_w3(1, 8)
@@ -185,48 +181,48 @@ def tile_list_mould_cycle_gap_kernel(
         tab2_picked = [held([P, W], U32, "tab2_picked%d" % half) for half in range(2)]
         nc.vector.tensor_copy(tab2_picked[0][:], tab2_window[:].indirect(list1_halves[0]))
         nc.vector.tensor_copy(tab2_picked[1][:], tab2_window[:].indirect(list1_halves[1]))
-        pass1_picked.append(tenant([P, W], U32, "pass1_picked1", 4))
-        nc.vector.tensor_copy(pass1_picked[1][:], tab_windows[1][:].indirect(list8_halves[1]))
-        tab_picked[1, 1] = pass1_picked[1][:]
 
         def difference_passes(b, half, t):
-            acc = bank([P, W], "difference%d%d%d" % (b, half, t), t)
+            group = 8 * b + 4 * half + t
+            acc = bank([P, W], "difference%d" % group, (group - 1) % 7 if group else 7)
             entries = slice(W * half, W * (half + 1))
             features = slice(P * t, P * (t + 1))
             first = W * b + P * t
 
-            def w1_pass(a):
+            def w1_pass(a, start, stop):
                 codes, plane = w1_mx[a, b]
                 nc.tensor.matmul_mx(
                     out=acc[:],
                     lhsT=codes[:, features].bitcast(FP8X4),
                     lhsT_scale=plane[:, features],
-                    rhs=tab_picked[a, half].bitcast(FP8X4),
+                    rhs=tab_picked[a][:, entries].bitcast(FP8X4),
                     rhs_scale=tab_planes[8 * a : P, entries],
-                    start=(a == 0),
-                    stop=False,
+                    start=start,
+                    stop=stop,
                 )
 
-            def w4_pass():
+            def w4_pass(start, stop):
                 nc.tensor.matmul_mx(
                     out=acc[:],
                     lhsT=w4_codes[:, 2 * first : 2 * (first + P)].bitcast(FP4X4),
                     lhsT_scale=w4_plane[:, first : first + P],
                     rhs=tab2_picked[half][:].bitcast(FP8X4),
                     rhs_scale=tab_planes[:, S + W * half : S + W * (half + 1)],
-                    start=False,
-                    stop=True,
+                    start=start,
+                    stop=stop,
                 )
 
-            return acc, [lambda: w1_pass(0), lambda: w1_pass(1), w4_pass]
+            if group < 4:
+                return acc, [lambda: w1_pass(0, True, False), lambda: w1_pass(1, False, False), lambda: w4_pass(False, True)]
+            return acc, [lambda: w4_pass(True, False), lambda: w1_pass(0, False, False), lambda: w1_pass(1, False, True)]
 
-        y_banks = [4, 5, 6, 0, 1, 2, 3, 4]
         gaps = {}
         acts = {}
         h_mx = {}
+        grouped_places = {(0, 0): (2, 0), (0, 1): (6, GROUPED_BYTES), (1, 0): (7, 0), (1, 1): (1, GROUPED_BYTES)}
 
         def activate(b, half, early=0):
-            gap = held([P, 4, W], F32, "gap%d%d" % (b, half))
+            gap = tenant([P, 4, W], F32, "gap%d%d" % (b, half), 9 + 2 * b + half)
             groups = [difference_passes(b, half, t) for t in range(4)]
             for step in range(early):
                 for acc, passes in groups:
@@ -245,19 +241,51 @@ def tile_list_mould_cycle_gap_kernel(
             gaps[b, half] = gap
             acts[b, half] = act
 
-        def quantise_h(b, half, pieces):
-            grouped = tenant([P, W, 4], BF16, "h_grouped%d%d" % (b, half), 6 + b, GROUPED_BYTES * half)
+        def activate_first(plain):
+            gap = tenant([P, 4, W], F32, "gap00", 9)
+            act = ring.tile([P, 4, W], F32, name="act", align_bytes=64)
+            groups = [difference_passes(0, 0, t) for t in range(4)]
+            for step in range(2):
+                for acc, passes in groups:
+                    passes[step]()
+            for t, (acc, passes) in enumerate(groups):
+                passes[2]()
+                if t < plain:
+                    nc.scalar.activation(out=gap[:, t, :], in_=acc[:], func=ACT.Abs)
+                else:
+                    nc.scalar.activation(
+                        out=act[:, t, :], in_=acc[:], func=ACT.Gelu_apprx_tanh, bias=zero_bias[:], scale=-1.0
+                    )
+                    nc.vector.scalar_tensor_tensor(act[:, t, :], acc[:], 0.0, act[:, t, :], ALU.max, ALU.add)
+            nc.scalar.activation(
+                out=act[:, :plain, :], in_=gap[:, :plain, :], func=ACT.Gelu_apprx_tanh, bias=zero_bias[:]
+            )
+            gaps[0, 0] = gap
+            acts[0, 0] = act
+
+        def quantise_h(b, half, pieces, between=None):
+            grouped = tenant([P, W, 4], BF16, "h_grouped%d%d" % (b, half), *grouped_places[b, half])
             codes = held([P, W], U32, "h_codes%d%d" % (b, half))
             plane = held([P, W], U8, "h_plane%d%d" % (b, half))
             gains = gain_columns[:, 4 * b : 4 * b + 4].rearrange("p (u e) -> p u e", e=2)
             for start, width in pieces:
                 n = slice(start, start + width)
-                nc.vector.tensor_tensor(
-                    grouped[:, n, :].rearrange("p n (u e) -> p n u e", e=2),
-                    acts[b, half][:, :, n, :].rearrange("p u n e -> p n u e"),
-                    gains.unsqueeze(1).to_broadcast([P, width, 2, 2]),
-                    ALU.mult,
-                )
+                if b + half > 0:
+                    nc.vector.tensor_tensor(
+                        grouped[:, n, :].rearrange("p n (u e) -> p n u e", e=2),
+                        acts[b, half][:, :, n, :].rearrange("p u n e -> p n u e"),
+                        gains.unsqueeze(1).to_broadcast([P, width, 2, 2]),
+                        ALU.mult,
+                    )
+                else:
+                    nc.vector.tensor_tensor(
+                        grouped[:, n, :].rearrange("p (c i) t -> p c t i", i=2),
+                        acts[b, half][:, :, n].rearrange("p t (c i) -> p c t i", i=2),
+                        gain_columns[:, 4 * b : 4 * b + 4].unsqueeze(1).unsqueeze(3).to_broadcast([P, width // 2, 4, 2]),
+                        ALU.mult,
+                    )
+                if between:
+                    between()
                 nc.vector.quantize_mx(
                     out=codes[:, n].bitcast(FP8X4),
                     scales=plane[:, n],
@@ -265,46 +293,59 @@ def tile_list_mould_cycle_gap_kernel(
                 )
             h_mx[b, half] = codes, plane
 
-        def defect_codes(half, start, width, staged):
+        def open_codes(half, start, width, n0, index):
+            acc = bank([P, W // width, width], "y%d%d%d" % (half, start, n0), index)
+            fill = (acc, half, start, width, n0)
+            codes_passes(fill, 0)
+            return fill
+
+        def codes_passes(fill, b):
+            acc, half, start, width, n0 = fill
             per_bank = W // width
             entries = slice(start, start + width)
-            for n0 in range(0, 4, per_bank):
-                acc = bank([P, per_bank, width], "y%d%d%d" % (half, start, n0), y_banks.pop(0))
-                for b in range(2):
-                    for x in range(per_bank):
-                        rows = slice(P * (n0 + x), P * (n0 + x + 1))
-                        nc.tensor.matmul_mx(
-                            out=acc[:, x, :],
-                            lhsT=w3_mx[b][0][:, rows].bitcast(FP8X4),
-                            lhsT_scale=w3_mx[b][1][:, rows],
-                            rhs=h_mx[b, half][0][:, entries].bitcast(FP8X4),
-                            rhs_scale=h_mx[b, half][1][:, entries],
-                            start=(b == 0 and x == 0),
-                            stop=(b == 1 and x == per_bank - 1),
-                        )
-                part = staged[:, width * n0 : width * n0 + W]
-                nc.scalar.activation(out=part, in_=acc[:].rearrange("p x n -> p (x n)"), func=ACT.Silu)
-                dst = out[P * n0 : P * (n0 + per_bank), W * half + start : W * half + start + width]
-                nc.sync.dma_start(
-                    out=dst.rearrange("(x p) n -> p x n", p=P), in_=part.rearrange("p (x n) -> p x n", n=width)
+            for x in range(per_bank):
+                rows = slice(P * (n0 + x), P * (n0 + x + 1))
+                nc.tensor.matmul_mx(
+                    out=acc[:, x, :],
+                    lhsT=w3_mx[b][0][:, rows].bitcast(FP8X4),
+                    lhsT_scale=w3_mx[b][1][:, rows],
+                    rhs=h_mx[b, half][0][:, entries].bitcast(FP8X4),
+                    rhs_scale=h_mx[b, half][1][:, entries],
+                    start=(b == 0 and x == 0),
+                    stop=(b == 1 and x == per_bank - 1),
                 )
+
+        def close_codes(fill, staged):
+            acc, half, start, width, n0 = fill
+            codes_passes(fill, 1)
+            nc.scalar.activation(out=staged, in_=acc[:].rearrange("p x n -> p (x n)"), func=ACT.Silu, bias=silu_bias[:])
+            dst = out[P * n0 : P * (n0 + W // width), W * half + start : W * half + start + width]
+            nc.sync.dma_start(
+                out=dst.rearrange("(x p) n -> p x n", p=P), in_=staged.rearrange("p (x n) -> p x n", n=width)
+            )
 
         w1_mx[0, 1] = prepare_w1(0, 1, tenant([P, 4 * W], BF16, "w1_grouped2", 6, GROUPED_BYTES), 0)
         w1_mx[1, 1] = prepare_w1(1, 1, tenant([P, 4 * W], BF16, "w1_grouped3", 6), 0)
-        activate(0, 0, 2)
+        activate_first(2)
         gain_columns = bank([P, P], "gain_columns", 7)
         nc.tensor.transpose(gain_columns[:], gain_rows[:], ident[:])
         quantise_h(0, 0, WHOLE)
-        w3_mx = [prepare_w3(0)]
+        w3_mx = [quantise("w3_0", round_w3(0)[:])]
         activate(0, 1)
         quantise_h(0, 1, WHOLE)
-        w3_mx.append(prepare_w3(1))
+        w3_last = round_w3(1)
         activate(1, 0)
-        quantise_h(1, 0, WHOLE)
+        w3_last_codes = tenant([P, W], U32, "w3_last_codes", 11)
+        quantise_h(1, 0, WHOLE, lambda: w3_mx.append(quantise("w3_1", w3_last[:], w3_last_codes)))
         activate(1, 1)
         quantise_h(1, 1, LAST_PIECES)
-        staged_first = held([P, 4 * W], F32, "gap11")
-        defect_codes(0, 0, W, staged_first[:])
-        staged_second = gaps[1, 0][:].rearrange("p t n -> p (t n)")
-        for start, width in LAST_PIECES:
-            defect_codes(1, start, width, staged_second[:, 4 * start : 4 * (start + width)])
+        silu_bias = tenant([P, 1], F32, "silu_bias", 12, 3 * BANK_BYTES)
+        nc.scalar.activation(out=silu_bias[:], in_=zero_bias[:], func=ACT.Silu)
+        staged_first = gaps[0, 0][:].rearrange("p t n -> p (t n)")
+        first = [open_codes(0, 0, W, n0, 1 + n0) for n0 in range(4)]
+        second = [open_codes(1, 0, 256, 0, 5), open_codes(1, 0, 256, 2, 6), open_codes(1, 256, 256, 0, 0)]
+        for n0 in range(4):
+            close_codes(first[n0], staged_first[:, W * n0 : W * (n0 + 1)])
+        second.append(open_codes(1, 256, 256, 2, 1))
+        for x in range(4):
+            close_codes(second[x], gaps[0, 1][:, x, :])

@@ -22,6 +22,7 @@ W = 512
 HALF_COLUMNS = W // 16
 BANK_BYTES = 4 * W
 ROOM_BYTES = 9216
+PLAIN_TILES = (2, 2, 4, 4)
 WHOLE = ((0, W),)
 LAST_PIECES = ((0, 256), (256, 256))
 GROUPED_BYTES = 2 * 4 * W
@@ -160,11 +161,12 @@ def tile_list_mould_cycle_gap_kernel(
             return quantise("w1_%d%d" % (a, b), grouped[:])
 
         def round_w3(b):
-            grouped = tenant([P, 4 * N], BF16, "w3_grouped%d" % b, 1, GROUPED_BYTES * b)
-            nc.vector.tensor_copy(
-                grouped[:].rearrange("p (c i t) -> p c t i", i=4, t=4),
-                w3_raw[b][:].rearrange("p t (c i) -> p c t i", i=4),
-            )
+            grouped = tenant([P, 4 * N], BF16, "w3_grouped%d" % b, 6)
+            src = w3_raw[b][:].rearrange("p t n -> p n t")
+            dst = grouped[:].rearrange("p (n t) -> p n t", t=4)
+            for n0 in range(4):
+                n = slice(P * n0, P * (n0 + 1))
+                nc.gpsimd.tensor_scalar(dst[:, n, :], src[:, n, :], 1.0, 0.0, ALU.mult, ALU.add)
             return grouped
 
         w1_mx = {}
@@ -219,10 +221,13 @@ def tile_list_mould_cycle_gap_kernel(
         gaps = {}
         acts = {}
         h_mx = {}
-        grouped_places = {(0, 0): (2, 0), (0, 1): (6, GROUPED_BYTES), (1, 0): (7, 0), (1, 1): (1, GROUPED_BYTES)}
+        grouped_places = {(0, 0): (2, 0), (0, 1): (6, GROUPED_BYTES), (1, 0): (7, 0), (1, 1): (6, 0)}
 
         def activate(b, half, early=0):
+            plain = PLAIN_TILES[2 * b + half]
             gap = tenant([P, 4, W], F32, "gap%d%d" % (b, half), 9 + 2 * b + half)
+            act = ring.tile([P, 4 * W], F32, name="act", align_bytes=64)
+            tiles = act[:].rearrange("p (t n) -> p t n", t=4)
             groups = [difference_passes(b, half, t) for t in range(4)]
             for step in range(early):
                 for acc, passes in groups:
@@ -230,38 +235,26 @@ def tile_list_mould_cycle_gap_kernel(
             for t, (acc, passes) in enumerate(groups):
                 for one_pass in passes[early:]:
                     one_pass()
-                nc.scalar.activation(out=gap[:, t, :], in_=acc[:], func=ACT.Abs)
-            act = ring.tile([P, 2, W, 2], F32, name="act", align_bytes=64)
-            nc.scalar.activation(
-                out=act[:],
-                in_=gap[:].rearrange("p (u e) n -> p u n e", e=2),
-                func=ACT.Gelu_apprx_tanh,
-                bias=zero_bias[:],
-            )
-            gaps[b, half] = gap
-            acts[b, half] = act
-
-        def activate_first(plain):
-            gap = tenant([P, 4, W], F32, "gap00", 9)
-            act = ring.tile([P, 4, W], F32, name="act", align_bytes=64)
-            groups = [difference_passes(0, 0, t) for t in range(4)]
-            for step in range(2):
-                for acc, passes in groups:
-                    passes[step]()
-            for t, (acc, passes) in enumerate(groups):
-                passes[2]()
                 if t < plain:
                     nc.scalar.activation(out=gap[:, t, :], in_=acc[:], func=ACT.Abs)
                 else:
                     nc.scalar.activation(
-                        out=act[:, t, :], in_=acc[:], func=ACT.Gelu_apprx_tanh, bias=zero_bias[:], scale=-1.0
+                        out=tiles[:, t, :], in_=acc[:], func=ACT.Gelu_apprx_tanh, bias=zero_bias[:], scale=-1.0
                     )
-                    nc.vector.scalar_tensor_tensor(act[:, t, :], acc[:], 0.0, act[:, t, :], ALU.max, ALU.add)
-            nc.scalar.activation(
-                out=act[:, :plain, :], in_=gap[:, :plain, :], func=ACT.Gelu_apprx_tanh, bias=zero_bias[:]
-            )
-            gaps[0, 0] = gap
-            acts[0, 0] = act
+                    nc.vector.scalar_tensor_tensor(tiles[:, t, :], acc[:], 0.0, tiles[:, t, :], ALU.max, ALU.add)
+            if plain == 4:
+                nc.scalar.activation(
+                    out=act[:].rearrange("p (u n e) -> p u n e", u=2, e=2),
+                    in_=gap[:].rearrange("p (u e) n -> p u n e", e=2),
+                    func=ACT.Gelu_apprx_tanh,
+                    bias=zero_bias[:],
+                )
+            elif plain:
+                nc.scalar.activation(
+                    out=tiles[:, :plain, :], in_=gap[:, :plain, :], func=ACT.Gelu_apprx_tanh, bias=zero_bias[:]
+                )
+            gaps[b, half] = gap
+            acts[b, half] = act
 
         def quantise_h(b, half, pieces, between=None):
             grouped = tenant([P, W, 4], BF16, "h_grouped%d%d" % (b, half), *grouped_places[b, half])
@@ -270,17 +263,17 @@ def tile_list_mould_cycle_gap_kernel(
             gains = gain_columns[:, 4 * b : 4 * b + 4].rearrange("p (u e) -> p u e", e=2)
             for start, width in pieces:
                 n = slice(start, start + width)
-                if b + half > 0:
+                if PLAIN_TILES[2 * b + half] == 4:
                     nc.vector.tensor_tensor(
                         grouped[:, n, :].rearrange("p n (u e) -> p n u e", e=2),
-                        acts[b, half][:, :, n, :].rearrange("p u n e -> p n u e"),
+                        acts[b, half][:].rearrange("p (u n e) -> p n u e", u=2, e=2)[:, n],
                         gains.unsqueeze(1).to_broadcast([P, width, 2, 2]),
                         ALU.mult,
                     )
                 else:
                     nc.vector.tensor_tensor(
                         grouped[:, n, :].rearrange("p (c i) t -> p c t i", i=2),
-                        acts[b, half][:, :, n].rearrange("p t (c i) -> p c t i", i=2),
+                        acts[b, half][:].rearrange("p (t n) -> p t n", t=4)[:, :, n].rearrange("p t (c i) -> p c t i", i=2),
                         gain_columns[:, 4 * b : 4 * b + 4].unsqueeze(1).unsqueeze(3).to_broadcast([P, width // 2, 4, 2]),
                         ALU.mult,
                     )
@@ -326,12 +319,13 @@ def tile_list_mould_cycle_gap_kernel(
 
         w1_mx[0, 1] = prepare_w1(0, 1, tenant([P, 4 * W], BF16, "w1_grouped2", 6, GROUPED_BYTES), 0)
         w1_mx[1, 1] = prepare_w1(1, 1, tenant([P, 4 * W], BF16, "w1_grouped3", 6), 0)
-        activate_first(2)
+        activate(0, 0, 2)
         gain_columns = bank([P, P], "gain_columns", 7)
         nc.tensor.transpose(gain_columns[:], gain_rows[:], ident[:])
-        quantise_h(0, 0, WHOLE)
-        w3_mx = [quantise("w3_0", round_w3(0)[:])]
+        w3_first = round_w3(0)
         activate(0, 1)
+        quantise_h(0, 0, WHOLE)
+        w3_mx = [quantise("w3_0", w3_first[:])]
         quantise_h(0, 1, WHOLE)
         w3_last = round_w3(1)
         activate(1, 0)

@@ -22,10 +22,12 @@ W = 512
 HALF_COLUMNS = W // 16
 BANK_BYTES = 4 * W
 ROOM_BYTES = 9216
-PLAIN_TILES = (2, 2, 4, 4)
-WHOLE = ((0, W),)
-LAST_PIECES = ((0, 256), (256, 256))
 GROUPED_BYTES = 2 * 4 * W
+GAIN_BANK = 7
+PLAIN_TILES = 2
+WHOLE = ((0, W),)
+PIECE = W // 2
+LAST_PIECES = ((0, PIECE), (PIECE, PIECE))
 
 
 def tile_list_mould_cycle_gap_kernel(
@@ -43,9 +45,6 @@ def tile_list_mould_cycle_gap_kernel(
 
         def tenant(shape, dtype, name, room, skip=0):
             return rooms.tile(shape, dtype, name=name, offset=ROOM_BYTES * room + skip, align_bytes=64)
-
-        def late_grouped(shape, side):
-            return tenant(shape, BF16, "late_grouped%d" % side, 4, GROUPED_BYTES * side)
 
         def bank(shape, name, index):
             return psum.tile(shape, F32, name=name, offset=BANK_BYTES * index)
@@ -121,7 +120,7 @@ def tile_list_mould_cycle_gap_kernel(
         nc.vector.tensor_copy(tab_planes[:].bitcast(I32), scale_picked[:].bitcast(I32))
 
         def move_odd_rows(a):
-            columns = slice(0, (2 - a) * S)
+            columns = slice(0, S if a else 2 * S)
             for c in range(2):
                 nc.sync.dma_start(
                     out=tab_planes[8 * a + 2 + c : P : 32, columns].bitcast(I32),
@@ -143,40 +142,45 @@ def tile_list_mould_cycle_gap_kernel(
             w4_scale_raw[:].bitcast(I32).rearrange("p (b m t) -> p b t m", b=2, t=4),
         )
 
-        def quantise(name, grouped, codes=None):
-            if codes is None:
-                codes = held([P, W], U32, name + "_codes")
-            plane = held([P, W], U8, name + "_plane")
-            nc.vector.quantize_mx(out=codes[:].bitcast(FP8X4), scales=plane[:], in_=grouped)
-            return codes, plane
+        def mx_tiles(name):
+            return held([P, W], U32, name + "_codes"), held([P, W], U8, name + "_plane")
 
-        def prepare_w1(a, b, grouped, tiles_on_scalar):
+        def quantise(target, columns, grouped):
+            codes, plane = target
+            nc.vector.quantize_mx(out=codes[:, columns].bitcast(FP8X4), scales=plane[:, columns], in_=grouped)
+
+        def round_w1(a, b, grouped):
             src = w1_raw[a, b][:].rearrange("p j (m t i) -> p t m j i", t=4, i=4)
             dst = grouped[:].rearrange("p (t m i j) -> p t m j i", t=4, i=4, j=4)
             for t in range(4):
-                if t < tiles_on_scalar:
+                if b == 0:
                     nc.scalar.activation(out=dst[:, t], in_=src[:, t], func=ACT.Copy, scale=-1.0)
                 else:
                     nc.vector.tensor_scalar(dst[:, t], src[:, t], -1.0, None, ALU.mult)
-            return quantise("w1_%d%d" % (a, b), grouped[:])
-
-        def round_w3(b):
-            grouped = tenant([P, 4 * N], BF16, "w3_grouped%d" % b, 6)
-            src = w3_raw[b][:].rearrange("p t n -> p n t")
-            dst = grouped[:].rearrange("p (n t) -> p n t", t=4)
-            for n0 in range(4):
-                n = slice(P * n0, P * (n0 + 1))
-                nc.gpsimd.tensor_scalar(dst[:, n, :], src[:, n, :], 1.0, 0.0, ALU.mult, ALU.add)
             return grouped
 
+        def quantise_w1(a, b, grouped):
+            w1_mx[a, b] = mx_tiles("w1_%d%d" % (a, b))
+            quantise(w1_mx[a, b], slice(0, W), grouped[:])
+
+        def round_w3(b, columns, grouped):
+            nc.gpsimd.tensor_scalar(
+                grouped.rearrange("p (n t) -> p n t", t=4),
+                w3_raw[b][:, :, columns].rearrange("p t n -> p n t"),
+                1.0,
+                0.0,
+                ALU.mult,
+                ALU.add,
+            )
+
         w1_mx = {}
-        w1_mx[0, 0] = prepare_w1(0, 0, tenant([P, 4 * W], BF16, "w1_grouped0", 8), 4)
+        quantise_w1(0, 0, round_w1(0, 0, tenant([P, 4 * W], BF16, "w1_grouped00", 8)))
         load_w1(1, 1, 2)
         gain_rows = tenant([P, P], F32, "gain_rows", 0)
         nc.vector.memset(gain_rows[:], 0.0)
         for b in range(2):
             load_gain(b, gain_rows)
-        w1_mx[1, 0] = prepare_w1(1, 0, tenant([P, 4 * W], BF16, "w1_grouped1", 8, GROUPED_BYTES), 4)
+        quantise_w1(1, 0, round_w1(1, 0, tenant([P, 4 * W], BF16, "w1_grouped10", 8, GROUPED_BYTES)))
         load_w3(0, 3)
         load_w3(1, 8)
 
@@ -186,7 +190,7 @@ def tile_list_mould_cycle_gap_kernel(
 
         def difference_passes(b, half, t):
             group = 8 * b + 4 * half + t
-            acc = bank([P, W], "difference%d" % group, (group - 1) % 7 if group else 7)
+            acc = bank([P, W], "difference%d" % group, (group - 1) % GAIN_BANK if group else GAIN_BANK)
             entries = slice(W * half, W * (half + 1))
             features = slice(P * t, P * (t + 1))
             first = W * b + P * t
@@ -214,17 +218,25 @@ def tile_list_mould_cycle_gap_kernel(
                     stop=stop,
                 )
 
-            if group < 4:
-                return acc, [lambda: w1_pass(0, True, False), lambda: w1_pass(1, False, False), lambda: w4_pass(False, True)]
-            return acc, [lambda: w4_pass(True, False), lambda: w1_pass(0, False, False), lambda: w1_pass(1, False, True)]
+            if b + half == 0:
+                return acc, [
+                    lambda: w1_pass(0, True, False),
+                    lambda: w1_pass(1, False, False),
+                    lambda: w4_pass(False, True),
+                ]
+            return acc, [
+                lambda: w4_pass(True, False),
+                lambda: w1_pass(0, False, False),
+                lambda: w1_pass(1, False, True),
+            ]
 
         gaps = {}
         acts = {}
         h_mx = {}
-        grouped_places = {(0, 0): (2, 0), (0, 1): (6, GROUPED_BYTES), (1, 0): (7, 0), (1, 1): (6, 0)}
 
-        def activate(b, half, early=0):
-            plain = PLAIN_TILES[2 * b + half]
+        def activate(b, half, zero=0.0):
+            plain = 4 if b else PLAIN_TILES
+            early = 0 if b + half else 2
             gap = tenant([P, 4, W], F32, "gap%d%d" % (b, half), 9 + 2 * b + half)
             act = ring.tile([P, 4 * W], F32, name="act", align_bytes=64)
             tiles = act[:].rearrange("p (t n) -> p t n", t=4)
@@ -241,58 +253,56 @@ def tile_list_mould_cycle_gap_kernel(
                     nc.scalar.activation(
                         out=tiles[:, t, :], in_=acc[:], func=ACT.Gelu_apprx_tanh, bias=zero_bias[:], scale=-1.0
                     )
-                    nc.vector.scalar_tensor_tensor(tiles[:, t, :], acc[:], 0.0, tiles[:, t, :], ALU.max, ALU.add)
-            if plain == 4:
+                    nc.vector.scalar_tensor_tensor(tiles[:, t, :], acc[:], zero, tiles[:, t, :], ALU.max, ALU.add)
+            if b:
                 nc.scalar.activation(
                     out=act[:].rearrange("p (u n e) -> p u n e", u=2, e=2),
                     in_=gap[:].rearrange("p (u e) n -> p u n e", e=2),
                     func=ACT.Gelu_apprx_tanh,
                     bias=zero_bias[:],
                 )
-            elif plain:
+            else:
                 nc.scalar.activation(
                     out=tiles[:, :plain, :], in_=gap[:, :plain, :], func=ACT.Gelu_apprx_tanh, bias=zero_bias[:]
                 )
             gaps[b, half] = gap
             acts[b, half] = act
 
-        def quantise_h(b, half, pieces, between=None):
-            grouped = tenant([P, W, 4], BF16, "h_grouped%d%d" % (b, half), *grouped_places[b, half])
-            codes = held([P, W], U32, "h_codes%d%d" % (b, half))
-            plane = held([P, W], U8, "h_plane%d%d" % (b, half))
-            gains = gain_columns[:, 4 * b : 4 * b + 4].rearrange("p (u e) -> p u e", e=2)
+        def apply_gain(b, half, pieces, room, skip):
+            grouped = tenant([P, W, 4], BF16, "h_grouped%d%d" % (b, half), room, skip)
+            gains = gain_columns[:, 4 * b : 4 * b + 4]
             for start, width in pieces:
                 n = slice(start, start + width)
-                if PLAIN_TILES[2 * b + half] == 4:
+                if b:
                     nc.vector.tensor_tensor(
                         grouped[:, n, :].rearrange("p n (u e) -> p n u e", e=2),
                         acts[b, half][:].rearrange("p (u n e) -> p n u e", u=2, e=2)[:, n],
-                        gains.unsqueeze(1).to_broadcast([P, width, 2, 2]),
+                        gains.rearrange("p (u e) -> p u e", e=2).unsqueeze(1).to_broadcast([P, width, 2, 2]),
                         ALU.mult,
                     )
                 else:
+                    tiles = acts[b, half][:].rearrange("p (t n) -> p t n", t=4)
                     nc.vector.tensor_tensor(
                         grouped[:, n, :].rearrange("p (c i) t -> p c t i", i=2),
-                        acts[b, half][:].rearrange("p (t n) -> p t n", t=4)[:, :, n].rearrange("p t (c i) -> p c t i", i=2),
-                        gain_columns[:, 4 * b : 4 * b + 4].unsqueeze(1).unsqueeze(3).to_broadcast([P, width // 2, 4, 2]),
+                        tiles[:, :, n].rearrange("p t (c i) -> p c t i", i=2),
+                        gains.unsqueeze(1).unsqueeze(3).to_broadcast([P, width // 2, 4, 2]),
                         ALU.mult,
                     )
-                if between:
-                    between()
-                nc.vector.quantize_mx(
-                    out=codes[:, n].bitcast(FP8X4),
-                    scales=plane[:, n],
-                    in_=grouped[:, n, :].rearrange("p n t -> p (n t)"),
-                )
-            h_mx[b, half] = codes, plane
+            return grouped
 
-        def open_codes(half, start, width, n0, index):
+        def quantise_h(b, half, pieces, grouped):
+            h_mx[b, half] = mx_tiles("h%d%d" % (b, half))
+            for start, width in pieces:
+                n = slice(start, start + width)
+                quantise(h_mx[b, half], n, grouped[:, n, :].rearrange("p n t -> p (n t)"))
+
+        def open_result(half, start, width, n0, index):
             acc = bank([P, W // width, width], "y%d%d%d" % (half, start, n0), index)
             fill = (acc, half, start, width, n0)
-            codes_passes(fill, 0)
+            result_passes(fill, 0)
             return fill
 
-        def codes_passes(fill, b):
+        def result_passes(fill, b):
             acc, half, start, width, n0 = fill
             per_bank = W // width
             entries = slice(start, start + width)
@@ -308,38 +318,54 @@ def tile_list_mould_cycle_gap_kernel(
                     stop=(b == 1 and x == per_bank - 1),
                 )
 
-        def close_codes(fill, staged):
+        def close_result(fill, staged):
             acc, half, start, width, n0 = fill
-            codes_passes(fill, 1)
-            nc.scalar.activation(out=staged, in_=acc[:].rearrange("p x n -> p (x n)"), func=ACT.Silu, bias=silu_bias[:])
+            result_passes(fill, 1)
+            nc.scalar.activation(
+                out=staged, in_=acc[:].rearrange("p x n -> p (x n)"), func=ACT.Silu, bias=silu_bias[:]
+            )
             dst = out[P * n0 : P * (n0 + W // width), W * half + start : W * half + start + width]
             nc.sync.dma_start(
                 out=dst.rearrange("(x p) n -> p x n", p=P), in_=staged.rearrange("p (x n) -> p x n", n=width)
             )
 
-        w1_mx[0, 1] = prepare_w1(0, 1, tenant([P, 4 * W], BF16, "w1_grouped2", 6, GROUPED_BYTES), 0)
-        w1_mx[1, 1] = prepare_w1(1, 1, tenant([P, 4 * W], BF16, "w1_grouped3", 6), 0)
-        activate(0, 0, 2)
-        gain_columns = bank([P, P], "gain_columns", 7)
+        quantise_w1(0, 1, round_w1(0, 1, tenant([P, 4 * W], BF16, "w1_grouped01", 6, GROUPED_BYTES)))
+        last_w1 = round_w1(1, 1, tenant([P, 4 * W], BF16, "w1_grouped11", 6))
+        late_zero = tenant([P, 1], F32, "late_zero", 2)
+        nc.vector.memset(late_zero[:], 0.0)
+        quantise_w1(1, 1, last_w1)
+        activate(0, 0)
+        gain_columns = bank([P, P], "gain_columns", GAIN_BANK)
         nc.tensor.transpose(gain_columns[:], gain_rows[:], ident[:])
-        w3_first = round_w3(0)
-        activate(0, 1)
-        quantise_h(0, 0, WHOLE)
-        w3_mx = [quantise("w3_0", w3_first[:])]
-        quantise_h(0, 1, WHOLE)
-        w3_last = round_w3(1)
+
+        w3_mx = [mx_tiles("w3_%d" % b) for b in range(2)]
+        all_rows, first_rows, last_rows = slice(0, N), slice(0, N // 2), slice(N // 2, N)
+        w3_early = tenant([P, 4 * N + 2 * N], BF16, "w3_early", 6, GROUPED_BYTES // 2)
+        round_w3(0, all_rows, w3_early[:, : 4 * N])
+        round_w3(1, first_rows, w3_early[:, 4 * N :])
+        activate(0, 1, late_zero[:])
+        h_first = apply_gain(0, 0, WHOLE, 6, -GROUPED_BYTES // 2)
+        h_second = apply_gain(0, 1, WHOLE, 7, GROUPED_BYTES)
+        quantise_h(0, 0, WHOLE, h_first)
+        quantise(w3_mx[0], all_rows, w3_early[:, : 4 * N])
+        quantise(w3_mx[1], first_rows, w3_early[:, 4 * N :])
+        quantise_h(0, 1, WHOLE, h_second)
+        w3_late = tenant([P, 2 * N], BF16, "w3_late", 7, GROUPED_BYTES)
+        round_w3(1, last_rows, w3_late[:])
         activate(1, 0)
-        w3_last_codes = tenant([P, W], U32, "w3_last_codes", 11)
-        quantise_h(1, 0, WHOLE, lambda: w3_mx.append(quantise("w3_1", w3_last[:], w3_last_codes)))
+        h_third = apply_gain(1, 0, WHOLE, 7, 0)
+        quantise(w3_mx[1], last_rows, w3_late[:])
+        quantise_h(1, 0, WHOLE, h_third)
         activate(1, 1)
-        quantise_h(1, 1, LAST_PIECES)
+        quantise_h(1, 1, LAST_PIECES, apply_gain(1, 1, LAST_PIECES, 7, GROUPED_BYTES))
+
         silu_bias = tenant([P, 1], F32, "silu_bias", 12, 3 * BANK_BYTES)
         nc.scalar.activation(out=silu_bias[:], in_=zero_bias[:], func=ACT.Silu)
-        staged_first = gaps[0, 0][:].rearrange("p t n -> p (t n)")
-        first = [open_codes(0, 0, W, n0, 1 + n0) for n0 in range(4)]
-        second = [open_codes(1, 0, 256, 0, 5), open_codes(1, 0, 256, 2, 6), open_codes(1, 256, 256, 0, 0)]
+        first = [open_result(0, 0, W, n0, 1 + n0) for n0 in range(4)]
+        later = [(start, n0) for start, width in LAST_PIECES for n0 in (0, 2)]
+        second = [open_result(1, start, PIECE, n0, (5 + x) % GAIN_BANK) for x, (start, n0) in enumerate(later[:3])]
         for n0 in range(4):
-            close_codes(first[n0], staged_first[:, W * n0 : W * (n0 + 1)])
-        second.append(open_codes(1, 256, 256, 2, 1))
+            close_result(first[n0], gaps[0, 0][:, n0, :])
+        second.append(open_result(1, later[3][0], PIECE, later[3][1], 1))
         for x in range(4):
-            close_codes(second[x], gaps[0, 1][:, x, :])
+            close_result(second[x], gaps[0, 1][:, x, :])

@@ -24,7 +24,7 @@ BANK_BYTES = 4 * W
 ROOM_BYTES = 9216
 GROUPED_BYTES = 2 * 4 * W
 GAIN_BANK = 7
-PLAIN_TILES = 2
+PLAIN_TILES = {(0, 0): 2, (0, 1): 2, (1, 0): 3, (1, 1): 4}
 WHOLE = ((0, W),)
 PIECE = W // 2
 LAST_PIECES = ((0, PIECE), (PIECE, PIECE))
@@ -235,7 +235,8 @@ def tile_list_mould_cycle_gap_kernel(
         h_mx = {}
 
         def activate(b, half, zero=0.0):
-            plain = 4 if b else PLAIN_TILES
+            count = PLAIN_TILES[b, half]
+            plain = slice(4 - count, 4) if b else slice(0, count)
             early = 0 if b + half else 2
             gap = tenant([P, 4, W], F32, "gap%d%d" % (b, half), 9 + 2 * b + half)
             act = ring.tile([P, 4 * W], F32, name="act", align_bytes=64)
@@ -247,14 +248,14 @@ def tile_list_mould_cycle_gap_kernel(
             for t, (acc, passes) in enumerate(groups):
                 for one_pass in passes[early:]:
                     one_pass()
-                if t < plain:
+                if plain.start <= t < plain.stop:
                     nc.scalar.activation(out=gap[:, t, :], in_=acc[:], func=ACT.Abs)
                 else:
                     nc.scalar.activation(
                         out=tiles[:, t, :], in_=acc[:], func=ACT.Gelu_apprx_tanh, bias=zero_bias[:], scale=-1.0
                     )
                     nc.vector.scalar_tensor_tensor(tiles[:, t, :], acc[:], zero, tiles[:, t, :], ALU.max, ALU.add)
-            if b:
+            if count == 4:
                 nc.scalar.activation(
                     out=act[:].rearrange("p (u n e) -> p u n e", u=2, e=2),
                     in_=gap[:].rearrange("p (u e) n -> p u n e", e=2),
@@ -263,7 +264,7 @@ def tile_list_mould_cycle_gap_kernel(
                 )
             else:
                 nc.scalar.activation(
-                    out=tiles[:, :plain, :], in_=gap[:, :plain, :], func=ACT.Gelu_apprx_tanh, bias=zero_bias[:]
+                    out=tiles[:, plain, :], in_=gap[:, plain, :], func=ACT.Gelu_apprx_tanh, bias=zero_bias[:]
                 )
             gaps[b, half] = gap
             acts[b, half] = act
@@ -273,7 +274,7 @@ def tile_list_mould_cycle_gap_kernel(
             gains = gain_columns[:, 4 * b : 4 * b + 4]
             for start, width in pieces:
                 n = slice(start, start + width)
-                if b:
+                if PLAIN_TILES[b, half] == 4:
                     nc.vector.tensor_tensor(
                         grouped[:, n, :].rearrange("p n (u e) -> p n u e", e=2),
                         acts[b, half][:].rearrange("p (u n e) -> p n u e", u=2, e=2)[:, n],
@@ -345,6 +346,7 @@ def tile_list_mould_cycle_gap_kernel(
         round_w3(1, first_rows, w3_early[:, 4 * N :])
         activate(0, 1, late_zero[:])
         h_first = apply_gain(0, 0, WHOLE, 6, -GROUPED_BYTES // 2)
+        activate(1, 0)
         h_second = apply_gain(0, 1, WHOLE, 7, GROUPED_BYTES)
         quantise_h(0, 0, WHOLE, h_first)
         quantise(w3_mx[0], all_rows, w3_early[:, : 4 * N])
@@ -352,7 +354,6 @@ def tile_list_mould_cycle_gap_kernel(
         quantise_h(0, 1, WHOLE, h_second)
         w3_late = tenant([P, 2 * N], BF16, "w3_late", 7, GROUPED_BYTES)
         round_w3(1, last_rows, w3_late[:])
-        activate(1, 0)
         h_third = apply_gain(1, 0, WHOLE, 7, 0)
         quantise(w3_mx[1], last_rows, w3_late[:])
         quantise_h(1, 0, WHOLE, h_third)

@@ -24,10 +24,12 @@ BANK_BYTES = 4 * W
 ROOM_BYTES = 9216
 GROUPED_BYTES = 2 * 4 * W
 GAIN_BANK = 7
-PLAIN_TILES = {(0, 0): 2, (0, 1): 2, (1, 0): 3, (1, 1): 4}
+ALL_PLAIN = (0, 4 * W)
+PLAIN = {(0, 0): (0, 2 * W), (0, 1): (0, 2 * W), (1, 0): (W + W // 2, 4 * W), (1, 1): ALL_PLAIN}
 WHOLE = ((0, W),)
 PIECE = W // 2
-LAST_PIECES = ((0, PIECE), (PIECE, PIECE))
+FRONT, BACK = (0, PIECE), (PIECE, PIECE)
+BACK_CUTS = ((PIECE, PIECE // 2), (PIECE + PIECE // 2, PIECE // 2))
 
 
 def tile_list_mould_cycle_gap_kernel(
@@ -117,7 +119,8 @@ def tile_list_mould_cycle_gap_kernel(
         tab_planes = held([P, 2 * S], U8, "tab_planes")
         nc.vector.tensor_copy(scale_picked[:, :S], tab_scale_window[:].indirect(list8[:]))
         nc.vector.tensor_copy(scale_picked[:, S:], tab2_scale_window[:].indirect(list1[:]))
-        nc.vector.tensor_copy(tab_planes[:].bitcast(I32), scale_picked[:].bitcast(I32))
+        for columns in (slice(0, S), slice(S, 2 * S)):
+            nc.vector.tensor_copy(tab_planes[:, columns].bitcast(I32), scale_picked[:, columns].bitcast(I32))
 
         def move_odd_rows(a):
             columns = slice(0, S if a else 2 * S)
@@ -161,7 +164,9 @@ def tile_list_mould_cycle_gap_kernel(
 
         def quantise_w1(a, b, grouped):
             w1_mx[a, b] = mx_tiles("w1_%d%d" % (a, b))
-            quantise(w1_mx[a, b], slice(0, W), grouped[:])
+            width = W // 2 if b else W
+            for start in range(0, W, width):
+                quantise(w1_mx[a, b], slice(start, start + width), grouped[:, 4 * start : 4 * (start + width)])
 
         def round_w3(b, columns, grouped):
             nc.gpsimd.tensor_scalar(
@@ -177,7 +182,7 @@ def tile_list_mould_cycle_gap_kernel(
         quantise_w1(0, 0, round_w1(0, 0, tenant([P, 4 * W], BF16, "w1_grouped00", 8)))
         load_w1(1, 1, 2)
         gain_rows = tenant([P, P], F32, "gain_rows", 0)
-        nc.vector.memset(gain_rows[:], 0.0)
+        nc.gpsimd.memset(gain_rows[:], 0.0)
         for b in range(2):
             load_gain(b, gain_rows)
         quantise_w1(1, 0, round_w1(1, 0, tenant([P, 4 * W], BF16, "w1_grouped10", 8, GROUPED_BYTES)))
@@ -232,11 +237,10 @@ def tile_list_mould_cycle_gap_kernel(
 
         gaps = {}
         acts = {}
-        h_mx = {}
+        h_mx = {(b, half): mx_tiles("h%d%d" % (b, half)) for b in range(2) for half in range(2)}
 
         def activate(b, half, zero=0.0):
-            count = PLAIN_TILES[b, half]
-            plain = slice(4 - count, 4) if b else slice(0, count)
+            low, high = PLAIN[b, half]
             early = 0 if b + half else 2
             gap = tenant([P, 4, W], F32, "gap%d%d" % (b, half), 9 + 2 * b + half)
             act = ring.tile([P, 4 * W], F32, name="act", align_bytes=64)
@@ -248,14 +252,19 @@ def tile_list_mould_cycle_gap_kernel(
             for t, (acc, passes) in enumerate(groups):
                 for one_pass in passes[early:]:
                     one_pass()
-                if plain.start <= t < plain.stop:
-                    nc.scalar.activation(out=gap[:, t, :], in_=acc[:], func=ACT.Abs)
-                else:
+                begin = min(max(low - W * t, 0), W)
+                end = min(max(high - W * t, 0), W)
+                shared = slice(0, begin) if begin else slice(end, W)
+                if shared.start < shared.stop:
+                    part = tiles[:, t, shared]
                     nc.scalar.activation(
-                        out=tiles[:, t, :], in_=acc[:], func=ACT.Gelu_apprx_tanh, bias=zero_bias[:], scale=-1.0
+                        out=part, in_=acc[:, shared], func=ACT.Gelu_apprx_tanh, bias=zero_bias[:], scale=-1.0
                     )
-                    nc.vector.scalar_tensor_tensor(tiles[:, t, :], acc[:], zero, tiles[:, t, :], ALU.max, ALU.add)
-            if count == 4:
+                if begin < end:
+                    nc.scalar.activation(out=gap[:, t, begin:end], in_=acc[:, begin:end], func=ACT.Abs)
+                if shared.start < shared.stop:
+                    nc.vector.scalar_tensor_tensor(part, acc[:, shared], zero, part, ALU.max, ALU.add)
+            if PLAIN[b, half] == ALL_PLAIN:
                 nc.scalar.activation(
                     out=act[:].rearrange("p (u n e) -> p u n e", u=2, e=2),
                     in_=gap[:].rearrange("p (u e) n -> p u n e", e=2),
@@ -264,17 +273,22 @@ def tile_list_mould_cycle_gap_kernel(
                 )
             else:
                 nc.scalar.activation(
-                    out=tiles[:, plain, :], in_=gap[:, plain, :], func=ACT.Gelu_apprx_tanh, bias=zero_bias[:]
+                    out=act[:, low:high],
+                    in_=gap[:].rearrange("p t n -> p (t n)")[:, low:high],
+                    func=ACT.Gelu_apprx_tanh,
+                    bias=zero_bias[:],
                 )
             gaps[b, half] = gap
             acts[b, half] = act
 
-        def apply_gain(b, half, pieces, room, skip):
-            grouped = tenant([P, W, 4], BF16, "h_grouped%d%d" % (b, half), room, skip)
+        def h_tile(b, half, room, skip):
+            return tenant([P, W, 4], BF16, "h_grouped%d%d" % (b, half), room, skip)
+
+        def apply_gain(b, half, pieces, grouped):
             gains = gain_columns[:, 4 * b : 4 * b + 4]
             for start, width in pieces:
                 n = slice(start, start + width)
-                if PLAIN_TILES[b, half] == 4:
+                if PLAIN[b, half] == ALL_PLAIN:
                     nc.vector.tensor_tensor(
                         grouped[:, n, :].rearrange("p n (u e) -> p n u e", e=2),
                         acts[b, half][:].rearrange("p (u n e) -> p n u e", u=2, e=2)[:, n],
@@ -292,7 +306,6 @@ def tile_list_mould_cycle_gap_kernel(
             return grouped
 
         def quantise_h(b, half, pieces, grouped):
-            h_mx[b, half] = mx_tiles("h%d%d" % (b, half))
             for start, width in pieces:
                 n = slice(start, start + width)
                 quantise(h_mx[b, half], n, grouped[:, n, :].rearrange("p n t -> p (n t)"))
@@ -345,25 +358,30 @@ def tile_list_mould_cycle_gap_kernel(
         round_w3(0, all_rows, w3_early[:, : 4 * N])
         round_w3(1, first_rows, w3_early[:, 4 * N :])
         activate(0, 1, late_zero[:])
-        h_first = apply_gain(0, 0, WHOLE, 6, -GROUPED_BYTES // 2)
+        h_first = apply_gain(0, 0, WHOLE, h_tile(0, 0, 6, -GROUPED_BYTES // 2))
         activate(1, 0)
-        h_second = apply_gain(0, 1, WHOLE, 7, GROUPED_BYTES)
+        h_second = apply_gain(0, 1, WHOLE, h_tile(0, 1, 7, GROUPED_BYTES))
         quantise_h(0, 0, WHOLE, h_first)
         quantise(w3_mx[0], all_rows, w3_early[:, : 4 * N])
         quantise(w3_mx[1], first_rows, w3_early[:, 4 * N :])
-        quantise_h(0, 1, WHOLE, h_second)
-        w3_late = tenant([P, 2 * N], BF16, "w3_late", 7, GROUPED_BYTES)
+        w3_late = tenant([P, 2 * N], BF16, "w3_late", 6, GROUPED_BYTES // 2)
         round_w3(1, last_rows, w3_late[:])
-        h_third = apply_gain(1, 0, WHOLE, 7, 0)
+        h_third = apply_gain(1, 0, WHOLE, h_tile(1, 0, 7, 0))
+        quantise_h(0, 1, [FRONT], h_second)
         quantise(w3_mx[1], last_rows, w3_late[:])
         quantise_h(1, 0, WHOLE, h_third)
         activate(1, 1)
-        quantise_h(1, 1, LAST_PIECES, apply_gain(1, 1, LAST_PIECES, 7, GROUPED_BYTES))
+        h_last = h_tile(1, 1, 6, GROUPED_BYTES // 2)
+        apply_gain(1, 1, [FRONT], h_last)
+        quantise_h(0, 1, [BACK], h_second)
+        quantise_h(1, 1, [FRONT], h_last)
+        apply_gain(1, 1, BACK_CUTS, h_last)
+        quantise_h(1, 1, BACK_CUTS, h_last)
 
         silu_bias = tenant([P, 1], F32, "silu_bias", 12, 3 * BANK_BYTES)
         nc.scalar.activation(out=silu_bias[:], in_=zero_bias[:], func=ACT.Silu)
         first = [open_result(0, 0, W, n0, 1 + n0) for n0 in range(4)]
-        later = [(start, n0) for start, width in LAST_PIECES for n0 in (0, 2)]
+        later = [(start, n0) for start, width in (FRONT, BACK) for n0 in (0, 2)]
         second = [open_result(1, start, PIECE, n0, (5 + x) % GAIN_BANK) for x, (start, n0) in enumerate(later[:3])]
         for n0 in range(4):
             close_result(first[n0], gaps[0, 0][:, n0, :])

@@ -94,10 +94,11 @@ def tile_list_mould_cycle_gap_kernel(
             nc.sync.dma_start(out=gain_rows[4 * b : 4 * b + 4, :].rearrange("t (m i) -> t m i", i=4), in_=rows[b])
 
         nc.sync.dma_start(list8[:], offs)
+        nc.sync.dma_start(list1[:], offs2)
+        nc.sync.dma_start(out=w4_raw[:].bitcast(I32), in_=w4_words[0].bitcast(I32))
         tab_scale_rows = tab_scales.bitcast(I32).rearrange("a (g c) t -> c g a t", c=2)
         for c in range(2):
             nc.sync.dma_start(out=tab_scale_window[c:P:8, :].bitcast(I32), in_=tab_scale_rows[c])
-        nc.sync.dma_start(list1[:], offs2)
         tab2_scale_rows = tab2_scales[0].bitcast(I32).rearrange("(g c) t -> c g t", c=2)
         for c in range(2):
             nc.sync.dma_start(out=tab2_scale_window[c:P:16, :].bitcast(I32), in_=tab2_scale_rows[c])
@@ -106,13 +107,12 @@ def tile_list_mould_cycle_gap_kernel(
         for c in range(4):
             load_w4_scale_rows(c)
         load_w1(1, 0, 3)
-        nc.sync.dma_start(out=w4_raw[:].bitcast(I32), in_=w4_words[0].bitcast(I32))
         tab_windows.append(load_table(tab_words[1], "tab_pass1", 1))
 
         w4_codes = held([P, 2 * H], U8, "w4_codes")
-        nc.vector.tensor_copy(
-            w4_codes[:].bitcast(I32).rearrange("p (b t m x) -> p b t m x", b=2, t=4, x=2),
-            w4_raw[:].bitcast(I32).rearrange("p (b m t x) -> p b t m x", b=2, t=4, x=2),
+        nc.scalar.copy(
+            w4_codes[:].bitcast(U32).rearrange("p (b t m x) -> p b t m x", b=2, t=4, x=2),
+            w4_raw[:].bitcast(U32).rearrange("p (b m t x) -> p b t m x", b=2, t=4, x=2),
         )
 
         scale_picked = tenant([P, 2 * S], U8, "scale_picked", 4, 4 * T - S // 2)
@@ -140,9 +140,9 @@ def tile_list_mould_cycle_gap_kernel(
         load_w1(0, 1, 5)
         list1_halves = [list1[:, HALF_COLUMNS * half : HALF_COLUMNS * (half + 1)] for half in range(2)]
         w4_plane = held([P, H], U8, "w4_plane")
-        nc.vector.tensor_copy(
-            w4_plane[:].bitcast(I32).rearrange("p (b t m) -> p b t m", b=2, t=4),
-            w4_scale_raw[:].bitcast(I32).rearrange("p (b m t) -> p b t m", b=2, t=4),
+        nc.scalar.copy(
+            w4_plane[:].bitcast(U32).rearrange("p (b t m) -> p b t m", b=2, t=4),
+            w4_scale_raw[:].bitcast(U32).rearrange("p (b m t) -> p b t m", b=2, t=4),
         )
 
         def mx_tiles(name):
@@ -156,7 +156,7 @@ def tile_list_mould_cycle_gap_kernel(
             src = w1_raw[a, b][:].rearrange("p j (m t i) -> p t m j i", t=4, i=4)
             dst = grouped[:].rearrange("p (t m i j) -> p t m j i", t=4, i=4, j=4)
             for t in range(4):
-                if b == 0:
+                if b == 0 and (a, t) != (1, 3):
                     nc.scalar.activation(out=dst[:, t], in_=src[:, t], func=ACT.Copy, scale=-1.0)
                 else:
                     nc.vector.tensor_scalar(dst[:, t], src[:, t], -1.0, None, ALU.mult)
@@ -164,7 +164,7 @@ def tile_list_mould_cycle_gap_kernel(
 
         def quantise_w1(a, b, grouped):
             w1_mx[a, b] = mx_tiles("w1_%d%d" % (a, b))
-            width = W // 2 if b else W
+            width = W // 2 if a + b else W
             for start in range(0, W, width):
                 quantise(w1_mx[a, b], slice(start, start + width), grouped[:, 4 * start : 4 * (start + width)])
 

@@ -94,15 +94,15 @@ def tile_list_mould_cycle_gap_kernel(
             nc.sync.dma_start(out=gain_rows[4 * b : 4 * b + 4, :].rearrange("t (m i) -> t m i", i=4), in_=rows[b])
 
         nc.sync.dma_start(list8[:], offs)
-        nc.sync.dma_start(list1[:], offs2)
         nc.sync.dma_start(out=w4_raw[:].bitcast(I32), in_=w4_words[0].bitcast(I32))
         tab_scale_rows = tab_scales.bitcast(I32).rearrange("a (g c) t -> c g a t", c=2)
         for c in range(2):
             nc.sync.dma_start(out=tab_scale_window[c:P:8, :].bitcast(I32), in_=tab_scale_rows[c])
+        load_w1(0, 0, 2)
+        nc.sync.dma_start(list1[:], offs2)
         tab2_scale_rows = tab2_scales[0].bitcast(I32).rearrange("(g c) t -> c g t", c=2)
         for c in range(2):
             nc.sync.dma_start(out=tab2_scale_window[c:P:16, :].bitcast(I32), in_=tab2_scale_rows[c])
-        load_w1(0, 0, 2)
         tab_windows = [load_table(tab_words[0], "tab_pass0", 0)]
         for c in range(4):
             load_w4_scale_rows(c)
@@ -332,11 +332,11 @@ def tile_list_mould_cycle_gap_kernel(
                     stop=(b == 1 and x == per_bank - 1),
                 )
 
-        def close_result(fill, staged):
+        def close_result(fill, staged, bias):
             acc, half, start, width, n0 = fill
             result_passes(fill, 1)
             nc.scalar.activation(
-                out=staged, in_=acc[:].rearrange("p x n -> p (x n)"), func=ACT.Silu, bias=silu_bias[:]
+                out=staged, in_=acc[:].rearrange("p x n -> p (x n)"), func=ACT.Silu, bias=bias[:]
             )
             dst = out[P * n0 : P * (n0 + W // width), W * half + start : W * half + start + width]
             nc.sync.dma_start(
@@ -384,7 +384,7 @@ def tile_list_mould_cycle_gap_kernel(
         later = [(start, n0) for start, width in (FRONT, BACK) for n0 in (0, 2)]
         second = [open_result(1, start, PIECE, n0, (5 + x) % GAIN_BANK) for x, (start, n0) in enumerate(later[:3])]
         for n0 in range(4):
-            close_result(first[n0], gaps[0, 0][:, n0, :])
+            close_result(first[n0], gaps[0, 0][:, n0, :], zero_bias)
         second.append(open_result(1, later[3][0], PIECE, later[3][1], 1))
         for x in range(4):
-            close_result(second[x], gaps[0, 1][:, x, :])
+            close_result(second[x], gaps[0, 1][:, x, :], silu_bias)

@@ -265,12 +265,13 @@ def tile_list_mould_cycle_gap_kernel(
                 if shared.start < shared.stop:
                     nc.vector.scalar_tensor_tensor(part, acc[:, shared], zero, part, ALU.max, ALU.add)
             if PLAIN[b, half] == ALL_PLAIN:
-                nc.scalar.activation(
-                    out=act[:].rearrange("p (u n e) -> p u n e", u=2, e=2),
-                    in_=gap[:].rearrange("p (u e) n -> p u n e", e=2),
-                    func=ACT.Gelu_apprx_tanh,
-                    bias=zero_bias[:],
-                )
+                for start, width in (FRONT, BACK) if half else WHOLE:
+                    nc.scalar.activation(
+                        out=act[:, 4 * start : 4 * (start + width)].rearrange("p (u n e) -> p u n e", u=2, e=2),
+                        in_=gap[:].rearrange("p (u e) n -> p u n e", e=2)[:, :, start : start + width],
+                        func=ACT.Gelu_apprx_tanh,
+                        bias=zero_bias[:],
+                    )
             else:
                 nc.scalar.activation(
                     out=act[:, low:high],
@@ -289,9 +290,12 @@ def tile_list_mould_cycle_gap_kernel(
             for start, width in pieces:
                 n = slice(start, start + width)
                 if PLAIN[b, half] == ALL_PLAIN:
+                    run = PIECE if half else W
+                    first = start - start % run
+                    pairs = acts[b, half][:, 4 * first : 4 * (first + run)].rearrange("p (u n e) -> p n u e", u=2, e=2)
                     nc.vector.tensor_tensor(
                         grouped[:, n, :].rearrange("p n (u e) -> p n u e", e=2),
-                        acts[b, half][:].rearrange("p (u n e) -> p n u e", u=2, e=2)[:, n],
+                        pairs[:, start - first : start - first + width],
                         gains.rearrange("p (u e) -> p u e", e=2).unsqueeze(1).to_broadcast([P, width, 2, 2]),
                         ALU.mult,
                     )
@@ -360,7 +364,7 @@ def tile_list_mould_cycle_gap_kernel(
         activate(0, 1, late_zero[:])
         h_first = apply_gain(0, 0, WHOLE, h_tile(0, 0, 6, -GROUPED_BYTES // 2))
         activate(1, 0)
-        h_second = apply_gain(0, 1, WHOLE, h_tile(0, 1, 7, GROUPED_BYTES))
+        h_second = apply_gain(0, 1, [FRONT], h_tile(0, 1, 7, GROUPED_BYTES))
         quantise_h(0, 0, WHOLE, h_first)
         quantise(w3_mx[0], all_rows, w3_early[:, : 4 * N])
         quantise(w3_mx[1], first_rows, w3_early[:, 4 * N :])
@@ -368,23 +372,28 @@ def tile_list_mould_cycle_gap_kernel(
         round_w3(1, last_rows, w3_late[:])
         h_third = apply_gain(1, 0, WHOLE, h_tile(1, 0, 7, 0))
         quantise_h(0, 1, [FRONT], h_second)
-        quantise(w3_mx[1], last_rows, w3_late[:])
         quantise_h(1, 0, WHOLE, h_third)
+        quantise(w3_mx[1], last_rows, w3_late[:])
         activate(1, 1)
         h_last = h_tile(1, 1, 6, GROUPED_BYTES // 2)
         apply_gain(1, 1, [FRONT], h_last)
-        quantise_h(0, 1, [BACK], h_second)
+        apply_gain(0, 1, BACK_CUTS[:1], h_second)
         quantise_h(1, 1, [FRONT], h_last)
-        apply_gain(1, 1, BACK_CUTS, h_last)
-        quantise_h(1, 1, BACK_CUTS, h_last)
+        apply_gain(1, 1, BACK_CUTS[:1], h_last)
+        quantise_h(0, 1, BACK_CUTS[:1], h_second)
+        apply_gain(0, 1, BACK_CUTS[1:], h_second)
+        quantise_h(1, 1, BACK_CUTS[:1], h_last)
+        apply_gain(1, 1, BACK_CUTS[1:], h_last)
+        quantise_h(0, 1, BACK_CUTS[1:], h_second)
+        quantise_h(1, 1, BACK_CUTS[1:], h_last)
 
         silu_bias = tenant([P, 1], F32, "silu_bias", 12, 3 * BANK_BYTES)
         nc.scalar.activation(out=silu_bias[:], in_=zero_bias[:], func=ACT.Silu)
         first = [open_result(0, 0, W, n0, 1 + n0) for n0 in range(4)]
-        later = [(start, n0) for start, width in (FRONT, BACK) for n0 in (0, 2)]
-        second = [open_result(1, start, PIECE, n0, (5 + x) % GAIN_BANK) for x, (start, n0) in enumerate(later[:3])]
+        later = [FRONT + (0,), FRONT + (2,)] + [cut + (0,) for cut in BACK_CUTS]
+        second = [open_result(1, *later[x], (5 + x) % GAIN_BANK) for x in range(3)]
         for n0 in range(4):
             close_result(first[n0], gaps[0, 0][:, n0, :], zero_bias)
-        second.append(open_result(1, later[3][0], PIECE, later[3][1], 1))
-        for x in range(4):
+        for x in range(3):
             close_result(second[x], gaps[0, 1][:, x, :], silu_bias)
+        close_result(open_result(1, *later[3], 1), gaps[0, 1][:, 3, :], silu_bias)

from contextlib import ExitStack

import concourse.mybir as mybir
from concourse.masks import make_identity

K, K2, T, S, H, N = 1024, 512, 2048, 1024, 1024, 512
FLOPS = 2 * S * (K * H + K2 * H + H * N)

F32 = mybir.dt.float32
BF16 = mybir.dt.bfloat16
I32 = mybir.dt.int32
U32 = mybir.dt.uint32
U16 = mybir.dt.uint16
U8 = mybir.dt.uint8
FP8X4 = mybir.dt.float8_e4m3fn_x4
FP4X4 = mybir.dt.float4_e2m1fn_x4
ACT = mybir.ActivationFunctionType
ALU = mybir.AluOpType

P = 128
W = 512
HALF_COLUMNS = W // 16
BANK_BYTES = 4 * W
ROOM_BYTES = 9216
GROUPED_BYTES = 2 * 4 * W
GAIN_BANK = 7
ALL_PLAIN = (0, 4 * W)
PLAIN = {(0, 0): (0, 2 * W), (0, 1): (0, 2 * W), (1, 0): (W + W // 2, 4 * W), (1, 1): ALL_PLAIN}
WHOLE = ((0, W),)
PIECE = W // 2
FRONT, BACK = (0, PIECE), (PIECE, PIECE)
BACK_CUTS = ((PIECE, PIECE // 2), (PIECE + PIECE // 2, PIECE // 2))


def tile_list_mould_cycle_gap_kernel(
    tc, tab_words, tab_scales, tab2_words, tab2_scales, offs, offs2, w1, w4_words, w4_scales, gain, w3, out
):
    nc = tc.nc
    with ExitStack() as ctx:
        keep = ctx.enter_context(tc.tile_pool(name="keep", bufs=1))
        ring = ctx.enter_context(tc.tile_pool(name="ring", bufs=4))
        rooms = ctx.enter_context(tc.tile_pool(name="rooms", bufs=1))
        psum = ctx.enter_context(tc.psum_pool(name="psum", bufs=1))

        def held(shape, dtype, name):
            return keep.tile(shape, dtype, name=name, align_bytes=64)

        def tenant(shape, dtype, name, room, skip=0):
            return rooms.tile(shape, dtype, name=name, offset=ROOM_BYTES * room + skip, align_bytes=64)

        def bank(shape, name, index):
            return psum.tile(shape, F32, name=name, offset=BANK_BYTES * index)

        list8 = keep.tile([P, S // 16], U16, name="list8")
        list1 = keep.tile([P, S // 16], U16, name="list1")
        tab_scale_window = held([P, T], U8, "tab_scale_window")
        tab2_scale_window = held([P, T], U8, "tab2_scale_window")
        w4_raw = held([P, 2 * H], U8, "w4_raw")
        w4_scale_raw = held([P, H], U8, "w4_scale_raw")
        ident = held([P, P], F32, "ident")
        w1_raw = {}
        w3_raw = {}

        nc.gpsimd.memset(tab_scale_window[:].bitcast(I32), 0)
        nc.vector.memset(tab2_scale_window[:].bitcast(I32), 0)
        nc.gpsimd.memset(w4_scale_raw[:].bitcast(I32), 0)
        make_identity(nc, ident[:])
        zero_bias = held([P, 1], F32, "zero_bias")
        nc.gpsimd.memset(zero_bias[:], 0.0)
        nc.scalar.activation(out=zero_bias[:], in_=zero_bias[:], func=ACT.Gelu_apprx_tanh)

        def load_table(packed, name, room):
            window = tenant([P, T], U32, name, room)
            nc.sync.dma_start(out=window[:].bitcast(I32), in_=packed.rearrange("p t i -> p (t i)").bitcast(I32))
            return window

        def load_w1(a, b, room):
            w1_raw[a, b] = tenant([P, 4, W], F32, "w1_raw%d%d" % (a, b), room)
            rows = w1[W * a : W * (a + 1), W * b : W * (b + 1)]
            nc.sync.dma_start(out=w1_raw[a, b][:], in_=rows.rearrange("(p j) c -> p j c", j=4))

        def load_w3(b, room):
            w3_raw[b] = tenant([P, 4, N], F32, "w3_raw%d" % b, room)
            rows = w3.rearrange("(b m t i) n -> b t m i n", b=2, t=4, i=4)
            for t in range(4):
                nc.sync.dma_start(out=w3_raw[b][:, t, :], in_=rows[b, t])

        def load_w4_scale_rows(c):
            rows = w4_scales[0].bitcast(I32).rearrange("(d c) t -> c d t", c=4)
            nc.sync.dma_start(out=w4_scale_raw[c:P:32, :].bitcast(I32), in_=rows[c])

        def load_gain(b, gain_rows):
            rows = gain.rearrange("(b m t i) -> b t m i", b=2, t=4, i=4)
            nc.sync.dma_start(out=gain_rows[4 * b : 4 * b + 4, :].rearrange("t (m i) -> t m i", i=4), in_=rows[b])

        nc.sync.dma_start(list8[:], offs)
        nc.sync.dma_start(out=w4_raw[:].bitcast(I32), in_=w4_words[0].bitcast(I32))
        tab_scale_rows = tab_scales.bitcast(I32).rearrange("a (g c) t -> c g a t", c=2)
        for c in range(2):
            nc.sync.dma_start(out=tab_scale_window[c:P:8, :].bitcast(I32), in_=tab_scale_rows[c])
        load_w1(0, 0, 2)
        nc.sync.dma_start(list1[:], offs2)
        tab2_scale_rows = tab2_scales[0].bitcast(I32).rearrange("(g c) t -> c g t", c=2)
        for c in range(2):
            nc.sync.dma_start(out=tab2_scale_window[c:P:16, :].bitcast(I32), in_=tab2_scale_rows[c])
        tab_windows = [load_table(tab_words[0], "tab_pass0", 0)]
        for c in range(4):
            load_w4_scale_rows(c)
        load_w1(1, 0, 3)
        tab_windows.append(load_table(tab_words[1], "tab_pass1", 1))

        w4_codes = held([P, 2 * H], U8, "w4_codes")
        nc.scalar.copy(
            w4_codes[:].bitcast(U32).rearrange("p (b t m x) -> p b t m x", b=2, t=4, x=2),
            w4_raw[:].bitcast(U32).rearrange("p (b m t x) -> p b t m x", b=2, t=4, x=2),
        )

        scale_picked = tenant([P, 2 * S], U8, "scale_picked", 4, 4 * T - S // 2)
        tab_planes = held([P, 2 * S], U8, "tab_planes")
        nc.vector.tensor_copy(scale_picked[:, :S], tab_scale_window[:].indirect(list8[:]))
        nc.vector.tensor_copy(scale_picked[:, S:], tab2_scale_window[:].indirect(list1[:]))
        for columns in (slice(0, S), slice(S, 2 * S)):
            nc.vector.tensor_copy(tab_planes[:, columns].bitcast(I32), scale_picked[:, columns].bitcast(I32))

        def move_odd_rows(a):
            columns = slice(0, S if a else 2 * S)
            for c in range(2):
                nc.sync.dma_start(
                    out=tab_planes[8 * a + 2 + c : P : 32, columns].bitcast(I32),
                    in_=tab_planes[16 + 8 * a + c : P : 32, columns].bitcast(I32),
                )

        move_odd_rows(0)
        move_odd_rows(1)
        tab2_window = load_table(tab2_words[0], "tab2", 4)

        tab_picked = [held([P, S], U32, "tab_picked%d" % a) for a in range(2)]
        for a in range(2):
            nc.vector.tensor_copy(tab_picked[a][:], tab_windows[a][:].indirect(list8[:]))
        load_w1(0, 1, 5)
        list1_halves = [list1[:, HALF_COLUMNS * half : HALF_COLUMNS * (half + 1)] for half in range(2)]
        w4_plane = held([P, H], U8, "w4_plane")
        nc.scalar.copy(
            w4_plane[:].bitcast(U32).rearrange("p (b t m) -> p b t m", b=2, t=4),
            w4_scale_raw[:].bitcast(U32).rearrange("p (b m t) -> p b t m", b=2, t=4),
        )

        def mx_tiles(name):
            return held([P, W], U32, name + "_codes"), held([P, W], U8, name + "_plane")

        def quantise(target, columns, grouped):
            codes, plane = target
            nc.vector.quantize_mx(out=codes[:, columns].bitcast(FP8X4), scales=plane[:, columns], in_=grouped)

        def round_w1(a, b, grouped):
            src = w1_raw[a, b][:].rearrange("p j (m t i) -> p t m j i", t=4, i=4)
            dst = grouped[:].rearrange("p (t m i j) -> p t m j i", t=4, i=4, j=4)
            for t in range(4):
                if b == 0 and (a, t) != (1, 3):
                    nc.scalar.activation(out=dst[:, t], in_=src[:, t], func=ACT.Copy, scale=-1.0)
                else:
                    nc.vector.tensor_scalar(dst[:, t], src[:, t], -1.0, None, ALU.mult)
            return grouped

        def quantise_w1(a, b, grouped):
            w1_mx[a, b] = mx_tiles("w1_%d%d" % (a, b))
            width = W // 2 if a + b else W
            for start in range(0, W, width):
                quantise(w1_mx[a, b], slice(start, start + width), grouped[:, 4 * start : 4 * (start + width)])

        def round_w3(b, columns, grouped):
            nc.gpsimd.tensor_scalar(
                grouped.rearrange("p (n t) -> p n t", t=4),
                w3_raw[b][:, :, columns].rearrange("p t n -> p n t"),
                1.0,
                0.0,
                ALU.mult,
                ALU.add,
            )

        w1_mx = {}
        quantise_w1(0, 0, round_w1(0, 0, tenant([P, 4 * W], BF16, "w1_grouped00", 8)))
        load_w1(1, 1, 2)
        gain_rows = tenant([P, P], F32, "gain_rows", 0)
        nc.gpsimd.memset(gain_rows[:], 0.0)
        for b in range(2):
            load_gain(b, gain_rows)
        quantise_w1(1, 0, round_w1(1, 0, tenant([P, 4 * W], BF16, "w1_grouped10", 8, GROUPED_BYTES)))
        load_w3(0, 3)
        load_w3(1, 8)

        tab2_picked = [held([P, W], U32, "tab2_picked%d" % half) for half in range(2)]
        nc.vector.tensor_copy(tab2_picked[0][:], tab2_window[:].indirect(list1_halves[0]))
        nc.vector.tensor_copy(tab2_picked[1][:], tab2_window[:].indirect(list1_halves[1]))

        def difference_passes(b, half, t):
            group = 8 * b + 4 * half + t
            acc = bank([P, W], "difference%d" % group, (group - 1) % GAIN_BANK if group else GAIN_BANK)
            entries = slice(W * half, W * (half + 1))
            features = slice(P * t, P * (t + 1))
            first = W * b + P * t

            def w1_pass(a, start, stop):
                codes, plane = w1_mx[a, b]
                nc.tensor.matmul_mx(
                    out=acc[:],
                    lhsT=codes[:, features].bitcast(FP8X4),
                    lhsT_scale=plane[:, features],
                    rhs=tab_picked[a][:, entries].bitcast(FP8X4),
                    rhs_scale=tab_planes[8 * a : P, entries],
                    start=start,
                    stop=stop,
                )

            def w4_pass(start, stop):
                nc.tensor.matmul_mx(
                    out=acc[:],
                    lhsT=w4_codes[:, 2 * first : 2 * (first + P)].bitcast(FP4X4),
                    lhsT_scale=w4_plane[:, first : first + P],
                    rhs=tab2_picked[half][:].bitcast(FP8X4),
                    rhs_scale=tab_planes[:, S + W * half : S + W * (half + 1)],
                    start=start,
                    stop=stop,
                )

            if b + half == 0:
                return acc, [
                    lambda: w1_pass(0, True, False),
                    lambda: w1_pass(1, False, False),
                    lambda: w4_pass(False, True),
                ]
            return acc, [
                lambda: w4_pass(True, False),
                lambda: w1_pass(0, False, False),
                lambda: w1_pass(1, False, True),
            ]

        gaps = {}
        acts = {}
        h_mx = {(b, half): mx_tiles("h%d%d" % (b, half)) for b in range(2) for half in range(2)}

        def activate(b, half, zero=0.0):
            low, high = PLAIN[b, half]
            early = 0 if b + half else 2
            gap = tenant([P, 4, W], F32, "gap%d%d" % (b, half), 9 + 2 * b + half)
            act = ring.tile([P, 4 * W], F32, name="act", align_bytes=64)
            tiles = act[:].rearrange("p (t n) -> p t n", t=4)
            groups = [difference_passes(b, half, t) for t in range(4)]
            for step in range(early):
                for acc, passes in groups:
                    passes[step]()
            for t, (acc, passes) in enumerate(groups):
                for one_pass in passes[early:]:
                    one_pass()
                begin = min(max(low - W * t, 0), W)
                end = min(max(high - W * t, 0), W)
                shared = slice(0, begin) if begin else slice(end, W)
                if shared.start < shared.stop:
                    part = tiles[:, t, shared]
                    nc.scalar.activation(
                        out=part, in_=acc[:, shared], func=ACT.Gelu_apprx_tanh, bias=zero_bias[:], scale=-1.0
                    )
                if begin < end:
                    nc.scalar.activation(out=gap[:, t, begin:end], in_=acc[:, begin:end], func=ACT.Abs)
                if shared.start < shared.stop:
                    nc.vector.scalar_tensor_tensor(part, acc[:, shared], zero, part, ALU.max, ALU.add)
            if PLAIN[b, half] == ALL_PLAIN:
                for start, width in (FRONT, BACK) if half else WHOLE:
                    nc.scalar.activation(
                        out=act[:, 4 * start : 4 * (start + width)].rearrange("p (u n e) -> p u n e", u=2, e=2),
                        in_=gap[:].rearrange("p (u e) n -> p u n e", e=2)[:, :, start : start + width],
                        func=ACT.Gelu_apprx_tanh,
                        bias=zero_bias[:],
                    )
            else:
                nc.scalar.activation(
                    out=act[:, low:high],
                    in_=gap[:].rearrange("p t n -> p (t n)")[:, low:high],
                    func=ACT.Gelu_apprx_tanh,
                    bias=zero_bias[:],
                )
            gaps[b, half] = gap
            acts[b, half] = act

        def h_tile(b, half, room, skip):
            return tenant([P, W, 4], BF16, "h_grouped%d%d" % (b, half), room, skip)

        def apply_gain(b, half, pieces, grouped):
            gains = gain_columns[:, 4 * b : 4 * b + 4]
            for start, width in pieces:
                n = slice(start, start + width)
                if PLAIN[b, half] == ALL_PLAIN:
                    run = PIECE if half else W
                    first = start - start % run
                    pairs = acts[b, half][:, 4 * first : 4 * (first + run)].rearrange("p (u n e) -> p n u e", u=2, e=2)
                    nc.vector.tensor_tensor(
                        grouped[:, n, :].rearrange("p n (u e) -> p n u e", e=2),
                        pairs[:, start - first : start - first + width],
                        gains.rearrange("p (u e) -> p u e", e=2).unsqueeze(1).to_broadcast([P, width, 2, 2]),
                        ALU.mult,
                    )
                else:
                    tiles = acts[b, half][:].rearrange("p (t n) -> p t n", t=4)
                    nc.vector.tensor_tensor(
                        grouped[:, n, :].rearrange("p (c i) t -> p c t i", i=2),
                        tiles[:, :, n].rearrange("p t (c i) -> p c t i", i=2),
                        gains.unsqueeze(1).unsqueeze(3).to_broadcast([P, width // 2, 4, 2]),
                        ALU.mult,
                    )
            return grouped

        def quantise_h(b, half, pieces, grouped):
            for start, width in pieces:
                n = slice(start, start + width)
                quantise(h_mx[b, half], n, grouped[:, n, :].rearrange("p n t -> p (n t)"))

        def open_result(half, start, width, n0, index):
            acc = bank([P, W // width, width], "y%d%d%d" % (half, start, n0), index)
            fill = (acc, half, start, width, n0)
            result_passes(fill, 0)
            return fill

        def result_passes(fill, b):
            acc, half, start, width, n0 = fill
            per_bank = W // width
            entries = slice(start, start + width)
            for x in range(per_bank):
                rows = slice(P * (n0 + x), P * (n0 + x + 1))
                nc.tensor.matmul_mx(
                    out=acc[:, x, :],
                    lhsT=w3_mx[b][0][:, rows].bitcast(FP8X4),
                    lhsT_scale=w3_mx[b][1][:, rows],
                    rhs=h_mx[b, half][0][:, entries].bitcast(FP8X4),
                    rhs_scale=h_mx[b, half][1][:, entries],
                    start=(b == 0 and x == 0),
                    stop=(b == 1 and x == per_bank - 1),
                )

        def close_result(fill, staged, bias):
            acc, half, start, width, n0 = fill
            result_passes(fill, 1)
            nc.scalar.activation(
                out=staged, in_=acc[:].rearrange("p x n -> p (x n)"), func=ACT.Silu, bias=bias[:]
            )
            dst = out[P * n0 : P * (n0 + W // width), W * half + start : W * half + start + width]
            nc.sync.dma_start(
                out=dst.rearrange("(x p) n -> p x n", p=P), in_=staged.rearrange("p (x n) -> p x n", n=width)
            )

        quantise_w1(0, 1, round_w1(0, 1, tenant([P, 4 * W], BF16, "w1_grouped01", 6, GROUPED_BYTES)))
        last_w1 = round_w1(1, 1, tenant([P, 4 * W], BF16, "w1_grouped11", 6))
        late_zero = tenant([P, 1], F32, "late_zero", 2)
        nc.vector.memset(late_zero[:], 0.0)
        quantise_w1(1, 1, last_w1)
        activate(0, 0)
        gain_columns = bank([P, P], "gain_columns", GAIN_BANK)
        nc.tensor.transpose(gain_columns[:], gain_rows[:], ident[:])

        w3_mx = [mx_tiles("w3_%d" % b) for b in range(2)]
        all_rows, first_rows, last_rows = slice(0, N), slice(0, N // 2), slice(N // 2, N)
        w3_early = tenant([P, 4 * N + 2 * N], BF16, "w3_early", 6, GROUPED_BYTES // 2)
        round_w3(0, all_rows, w3_early[:, : 4 * N])
        round_w3(1, first_rows, w3_early[:, 4 * N :])
        activate(0, 1, late_zero[:])
        h_first = apply_gain(0, 0, WHOLE, h_tile(0, 0, 6, -GROUPED_BYTES // 2))
        activate(1, 0)
        h_second = apply_gain(0, 1, [FRONT], h_tile(0, 1, 7, GROUPED_BYTES))
        quantise_h(0, 0, WHOLE, h_first)
        quantise(w3_mx[0], all_rows, w3_early[:, : 4 * N])
        quantise(w3_mx[1], first_rows, w3_early[:, 4 * N :])
        w3_late = tenant([P, 2 * N], BF16, "w3_late", 6, GROUPED_BYTES // 2)
        round_w3(1, last_rows, w3_late[:])
        h_third = apply_gain(1, 0, WHOLE, h_tile(1, 0, 7, 0))
        quantise_h(0, 1, [FRONT], h_second)
        quantise_h(1, 0, WHOLE, h_third)
        quantise(w3_mx[1], last_rows, w3_late[:])
        activate(1, 1)
        h_last = h_tile(1, 1, 6, GROUPED_BYTES // 2)
        apply_gain(1, 1, [FRONT], h_last)
        apply_gain(0, 1, BACK_CUTS[:1], h_second)
        quantise_h(1, 1, [FRONT], h_last)
        apply_gain(1, 1, BACK_CUTS[:1], h_last)
        quantise_h(0, 1, BACK_CUTS[:1], h_second)
        apply_gain(0, 1, BACK_CUTS[1:], h_second)
        quantise_h(1, 1, BACK_CUTS[:1], h_last)
        apply_gain(1, 1, BACK_CUTS[1:], h_last)
        quantise_h(0, 1, BACK_CUTS[1:], h_second)
        quantise_h(1, 1, BACK_CUTS[1:], h_last)

        silu_bias = tenant([P, 1], F32, "silu_bias", 12, 3 * BANK_BYTES)
        nc.scalar.activation(out=silu_bias[:], in_=zero_bias[:], func=ACT.Silu)
        first = [open_result(0, 0, W, n0, 1 + n0) for n0 in range(4)]
        later = [FRONT + (0,), FRONT + (2,)] + [cut + (0,) for cut in BACK_CUTS]
        second = [open_result(1, *later[x], (5 + x) % GAIN_BANK) for x in range(3)]
        for n0 in range(4):
            close_result(first[n0], gaps[0, 0][:, n0, :], zero_bias)
        for x in range(3):
            close_result(second[x], gaps[0, 1][:, x, :], silu_bias)
        close_result(open_result(1, *later[3], 1), gaps[0, 1][:, 3, :], silu_bias)
